import numpy as np
import ml_dtypes


def mxq(x, axis, fmt="e4m3"):
    dtype, down = {"e4m3": (ml_dtypes.float8_e4m3fn, 7), "e5m2": (ml_dtypes.float8_e5m2, 14)}[fmt]
    v = np.moveaxis(np.asarray(x, np.float32).astype(ml_dtypes.bfloat16).astype(np.float64), axis, -1)
    blocks = v.reshape(v.shape[:-1] + (-1, 32))
    amax = np.abs(blocks).max(-1, keepdims=True)
    byte = np.maximum(np.where(amax > 0, np.frexp(amax)[1] - 1 + 127, 0) - down, 1)
    scale = np.exp2(byte - 127.0)
    codes = (blocks / scale).astype(np.float32).astype(dtype).astype(np.float64)
    return np.moveaxis((codes * scale).reshape(v.shape), -1, axis)


WIDE = False


def mx_kscale(k):
    if not WIDE:
        return np.ones(k)
    levels = np.array([10, -10, 5, -5, 0])
    if k % 512:
        return np.exp2(np.random.permutation(np.resize(levels, k // 32))).repeat(32)
    a = np.empty((k // 512, 16))
    for p in range(k // 512):
        a[p, :8] = np.random.permutation(np.resize(levels, 8))
        for g in range(8):
            far = levels[np.abs(levels - a[p, g]) >= 10]
            a[p, g + 8] = far[np.random.randint(len(far))]
    return np.exp2(a.ravel()).repeat(32)


def f64(x):
    return np.asarray(x).astype(np.float64)


def striped(idx):
    return np.tile(idx.reshape(-1, 16).T, (8, 1)).astype(np.uint16)


def unstriped(offs):
    return offs[:16].T.reshape(-1).astype(np.int64)


E2M1 = np.array([0.0, 0.5, 1.0, 1.5, 2.0, 3.0, 4.0, 6.0, -0.0, -0.5, -1.0, -1.5, -2.0, -3.0, -4.0, -6.0])


def pack_weight(w, fmt):
    k, n = w.shape
    w = f64(np.asarray(w, np.float32).astype(ml_dtypes.bfloat16)).reshape(k // 32, 32, n)
    amax = np.abs(w).max(1)
    if fmt == "e4m3":
        byte = np.frexp(amax)[1] - 1 + 127 - 7
    else:
        mant, ex = np.frexp(amax / 6.0)
        byte = np.where(mant > 0.5, ex, ex - 1) + 127
    byte = np.clip(np.where(amax > 0, byte, 1), 1, 254)
    scaled = (w * np.exp2(127.0 - byte)[:, None, :]).reshape(k, n).astype(np.float32)
    by_word = np.ascontiguousarray(scaled.reshape(k // 512, 128, 4, n).transpose(0, 1, 3, 2))
    if fmt == "e4m3":
        words = by_word.astype(ml_dtypes.float8_e4m3fn).view(np.uint8)
    else:
        c = by_word.astype(ml_dtypes.float4_e2m1fn).view(np.uint8) & 0xF
        words = (c[..., 0::2] | (c[..., 1::2] << 4)).reshape(k // 512, 128, 2 * n)
    return np.ascontiguousarray(words), np.ascontiguousarray(byte.astype(np.uint8).reshape(k // 512, 16, n))


def unpack_weight(words, scales, fmt):
    g, _, n = scales.shape
    words = np.ascontiguousarray(words).reshape(g, 128, n, -1)
    if fmt == "e4m3":
        vals = words.view(ml_dtypes.float8_e4m3fn).astype(np.float64)
    else:
        nib = np.empty((g, 128, n, 4), np.uint8)
        nib[..., 0::2] = words & 0xF
        nib[..., 1::2] = words >> 4
        vals = E2M1[nib]
    vals = vals * np.repeat(np.exp2(scales.astype(np.float64) - 127.0), 8, axis=1)[..., None]
    return vals.transpose(0, 1, 3, 2).reshape(g * 512, n)


def silu(v):
    return v / (1.0 + np.exp(-np.maximum(v, -700.0)))


K, T, S1, S2 = 512, 2048, 1024, 1024


def setup_inputs():
    n = np.random.standard_normal
    s = mx_kscale(K)
    u = mx_kscale(K)
    first, second = np.random.permutation(T)[:S1], np.random.permutation(T)[:S2]
    xf = n((K, T))
    x = pack_weight(xf * s[:, None], "e4m3")
    w2 = pack_weight(n((K, K)) / np.sqrt(K) / u[:, None] * u, "e4m3")
    return {
        "x_words": x[0],
        "x_scales": x[1],
        "xr": (xf * u[:, None]).astype(np.float32),
        "w1": (n((K, K)) / np.sqrt(K) / s[:, None] * u).astype(np.float32),
        "w2_words": w2[0],
        "w2_scales": w2[1],
        "gate1": (np.tile(np.random.uniform(0.2, 1.0, S1), (128, 1))).astype(np.float32),
        "gate2": (np.tile(np.random.uniform(0.2, 1.0, S2), (128, 1))).astype(np.float32),
        "offs": striped(first),
        "offs2": striped(second),
    }


def reference(x_words, x_scales, xr, w1, w2_words, w2_scales, gate1, gate2, offs, offs2):
    w1q = mxq(f64(w1), 0, "e4m3")
    w2 = unpack_weight(w2_words, w2_scales, "e4m3")
    idx, idx2 = unstriped(offs), unstriped(offs2)
    r = f64(xr)
    r[:, idx] += f64(gate1[:1]) * silu(w1q.T @ unpack_weight(x_words, x_scales, "e4m3")[:, idx])
    r2 = r.copy()
    r2[:, idx2] += f64(gate2[:1]) * silu(w2.T @ mxq(r[:, idx2], 0, "e4m3"))
    return r2

@@ -1,0 +1,200 @@
+from contextlib import ExitStack
+
+import concourse.mybir as mybir
+from concourse.masks import make_identity
+
+F32 = mybir.dt.float32
+BF16 = mybir.dt.bfloat16
+I32 = mybir.dt.int32
+U32 = mybir.dt.uint32
+U16 = mybir.dt.uint16
+U8 = mybir.dt.uint8
+FP8X4 = mybir.dt.float8_e4m3fn_x4
+MULT = mybir.AluOpType.mult
+ADD = mybir.AluOpType.add
+SILU = mybir.ActivationFunctionType.Silu
+
+P = 128
+K = 512
+T = 2048
+S = 1024
+PACK = 4
+CH = 256
+NCH = S // CH
+BANK = 512
+FLOPS = 2 * 2 * K * K * S
+
+
+def tile_moe_mod_silu_kernel(
+    tc, x_words, x_scales, xr, w1, w2_words, w2_scales, gate1, gate2, offs, offs2, out
+):
+    nc = tc.nc
+    with ExitStack() as ctx:
+        keep = ctx.enter_context(tc.tile_pool(name="keep", bufs=1))
+        ring = ctx.enter_context(tc.tile_pool(name="ring", bufs=3))
+        mm_ps = ctx.enter_context(tc.psum_pool(name="mm_ps", bufs=2))
+        a_ps = ctx.enter_context(tc.psum_pool(name="a_ps", bufs=3))
+        b_ps = ctx.enter_context(tc.psum_pool(name="b_ps", bufs=3))
+
+        def held(name, shape, dtype):
+            return keep.tile(shape, dtype, name=name, align_bytes=64)
+
+        idx1 = keep.tile([P, S // 16], U16, name="idx1")
+        idx2 = keep.tile([P, S // 16], U16, name="idx2")
+        xw = held("xw", [P, T], I32)
+        xs = held("xs", [P, T], U8)
+        w1_raw = held("w1_raw", [P, PACK, K], F32)
+        w1_bf = held("w1_bf", [P, K * PACK], BF16)
+        w1_q = held("w1_q", [P, K], U32)
+        w1_s = held("w1_s", [P, K], U8)
+        w2_raw = held("w2_raw", [P, K], I32)
+        w2s_raw = held("w2s_raw", [P, K], U8)
+        w2_q = held("w2_q", [P, K], I32)
+        w2_s = held("w2_s", [P, K], U8)
+        g1 = held("g1", [P, S], F32)
+        g2 = held("g2", [P, S], F32)
+        ident = held("ident", [P, P], F32)
+        warm = held("warm", [P, 8], F32)
+        res = [held(f"res{t}", [P, T], F32) for t in range(PACK)]
+        r = [held(f"r{t}", [P, T], F32) for t in range(PACK)]
+        spread = [held(f"spread{i}", [P, T], F32) for i in range(2)]
+        gw = [held(f"gw{c}", [P, CH], U32) for c in range(NCH)]
+        gs = [held(f"gs{c}", [P, CH], U8) for c in range(NCH)]
+        y = [held(f"y{t}", [P, S], F32) for t in range(PACK)]
+        z = [held(f"z{t}", [P, S], F32) for t in range(PACK)]
+        rg = [held(f"rg{c}", [P, PACK, CH], F32) for c in range(NCH)]
+        rb = [held(f"rb{c}", [P, CH * PACK], BF16) for c in range(NCH)]
+        rq = [held(f"rq{c}", [P, CH], U32) for c in range(NCH)]
+        rs = [held(f"rs{c}", [P, CH], U8) for c in range(NCH)]
+
+        xr_v = xr.rearrange("(p t) c -> p t c", t=PACK)
+        out_v = out.rearrange("(p t) c -> p t c", t=PACK)
+        w1_v = w1.rearrange("(p j) n -> p j n", j=PACK)
+
+        nc.vector.memset(xs[:].bitcast(I32), 0)
+        nc.sync.dma_start(idx1[:], offs)
+        nc.sync.dma_start(xw[:], x_words[0].rearrange("p c d -> p (c d)").bitcast(I32))
+        for q in range(4):
+            nc.scalar.dma_start(xs[32 * q : 32 * q + 4, :].bitcast(I32), x_scales[0, 4 * q : 4 * q + 4, :].bitcast(I32))
+        nc.vector.memset(warm[:], 0.0)
+        nc.scalar.activation(warm[:, 4:8], warm[:, 0:4], SILU)
+        for h in range(2):
+            nc.sync.dma_start(w1_raw[:, :, h * 256 : (h + 1) * 256], w1_v[:, :, h * 256 : (h + 1) * 256])
+        nc.sync.dma_start(g1[:], gate1)
+        nc.vector.memset(spread[0][:], 0.0)
+        nc.vector.memset(spread[1][:], 0.0)
+        nc.vector.memset(w2s_raw[:].bitcast(I32), 0)
+        make_identity(nc, ident[:])
+        for t in range(PACK):
+            nc.sync.dma_start(res[t][:], xr_v[:, t, :])
+        nc.sync.dma_start(idx2[:], offs2)
+        nc.sync.dma_start(w2_raw[:], w2_words[0].rearrange("p n d -> p (n d)").bitcast(I32))
+        for q in range(4):
+            nc.sync.dma_start(w2s_raw[32 * q : 32 * q + 4, :].bitcast(I32), w2_scales[0, 4 * q : 4 * q + 4, :].bitcast(I32))
+        nc.sync.dma_start(g2[:], gate2)
+
+        def cols(c):
+            return slice(c * CH, (c + 1) * CH)
+
+        def entries(idx, c):
+            return idx[:, c * CH // 16 : (c + 1) * CH // 16]
+
+        w1_dst = w1_bf[:].rearrange("p (t m j) -> p m t j", t=PACK, j=PACK)
+        w1_src = w1_raw[:].rearrange("p j (m t) -> p m t j", t=PACK)
+        for h in range(2):
+            nc.scalar.copy(w1_dst[:, h * 64 : (h + 1) * 64], w1_src[:, h * 64 : (h + 1) * 64])
+
+        def gather_tokens(c):
+            nc.vector.tensor_copy(gw[c][:], xw[:].bitcast(U32).indirect(entries(idx1, c)))
+            nc.vector.tensor_copy(gs[c][:], xs[:].indirect(entries(idx1, c)))
+
+        def product(wq, ws, codes, scales, dst, t, c0):
+            acc = mm_ps.tile([P, BANK], F32, name="acc")
+            for u in range(2):
+                nc.tensor.matmul_mx(
+                    out=acc[:, u * CH : (u + 1) * CH],
+                    lhsT=wq[:, t * P : (t + 1) * P].bitcast(FP8X4),
+                    lhsT_scale=ws[:, t * P : (t + 1) * P],
+                    rhs=codes[c0 + u][:].bitcast(FP8X4),
+                    rhs_scale=scales[c0 + u][:],
+                    start=True,
+                    stop=True,
+                )
+            nc.scalar.activation(dst[:, c0 * CH : (c0 + 2) * CH], acc[:], SILU)
+
+        for c in range(3):
+            gather_tokens(c)
+        nc.vector.quantize_mx(out=w1_q[:].bitcast(FP8X4), scales=w1_s[:], in_=w1_bf[:])
+        gather_tokens(3)
+        for t in range(PACK):
+            for c0 in (0, 2):
+                product(w1_q, w1_s, gw, gs, y[t], t, c0)
+
+        def add_by_transposes(t):
+            for g in range(T // BANK):
+                a = a_ps.tile([P, BANK], F32, name="a")
+                for b in range(4):
+                    blk = slice(g * BANK + b * P, g * BANK + (b + 1) * P)
+                    nc.tensor.matmul(a[:, b * P : (b + 1) * P], res[t][:, blk], ident[:], start=True, stop=False, is_transpose=True)
+                    nc.tensor.matmul(a[:, b * P : (b + 1) * P], spread[t % 2][:, blk], ident[:], start=False, stop=True, is_transpose=True)
+                turned = ring.tile([P, BANK], F32, name="turned")
+                nc.scalar.copy(turned[:], a[:])
+                bk = b_ps.tile([P, BANK], F32, name="bk")
+                for b in range(4):
+                    nc.tensor.transpose(bk[:, b * P : (b + 1) * P], turned[:, b * P : (b + 1) * P], ident[:])
+                nc.scalar.copy(r[t][:, g * BANK : (g + 1) * BANK], bk[:])
+
+        def gather_r(t, c):
+            nc.vector.tensor_copy(rg[c][:, t, :], r[t][:].indirect(entries(idx2, c)))
+
+        for t in range(PACK):
+            if t == 0:
+                for h in range(2):
+                    half = slice(h * 512, (h + 1) * 512)
+                    nc.vector.tensor_tensor(spread[0][:].indirect(idx1[:, h * 32 : (h + 1) * 32]), y[0][:, half], g1[:, half], MULT)
+            else:
+                nc.vector.tensor_tensor(spread[t % 2][:].indirect(idx1[:]), y[t][:], g1[:], MULT)
+            add_by_transposes(t)
+
+        nc.vector.tensor_copy(w2_q[:].rearrange("p (t m) -> p t m", t=PACK), w2_raw[:].rearrange("p (m t) -> p t m", t=PACK))
+        nc.vector.tensor_copy(w2_s[:].rearrange("p (t m) -> p t m", t=PACK), w2s_raw[:].rearrange("p (m t) -> p t m", t=PACK))
+        for c in range(3):
+            for t in range(3):
+                gather_r(t, c)
+
+        def round_r(c):
+            nc.scalar.copy(rb[c][:].rearrange("p (c t) -> p c t", t=PACK), rg[c][:].rearrange("p t c -> p c t"))
+
+        def quant_r(c):
+            nc.vector.quantize_mx(out=rq[c][:].bitcast(FP8X4), scales=rs[c][:], in_=rb[c][:])
+
+        gather_r(3, 0)
+        round_r(0)
+        gather_r(3, 1)
+        round_r(1)
+        gather_r(3, 2)
+        round_r(2)
+        for t in range(PACK):
+            gather_r(t, 3)
+            if t == 1:
+                quant_r(0)
+            if t == 3:
+                quant_r(1)
+        round_r(3)
+        for t in range(PACK):
+            product(w2_q, w2_s, rq, rs, z[t], t, 0)
+        quant_r(2)
+        quant_r(3)
+        for t in range(PACK):
+            product(w2_q, w2_s, rq, rs, z[t], t, 2)
+
+        for t in range(PACK):
+            for h in range(2):
+                half = slice(h * 512, (h + 1) * 512)
+                u = ring.tile([P, 512], F32, name="u")
+                v = ring.tile([P, 512], F32, name="v")
+                nc.vector.tensor_tensor(u[:], z[t][:, half], g2[:, half], MULT)
+                for e in range(2):
+                    nc.vector.tensor_tensor(v[:, e * CH : (e + 1) * CH], u[:, e * CH : (e + 1) * CH], rg[2 * h + e][:, t, :], ADD)
+                nc.vector.tensor_copy(r[t][:].indirect(idx2[:, h * 32 : (h + 1) * 32]), v[:])
+            nc.sync.dma_start(out_v[:, t, :], r[t][:])

@@ -13,15 +13,18 @@ FP8X4 = mybir.dt.float8_e4m3fn_x4
 MULT = mybir.AluOpType.mult
 ADD = mybir.AluOpType.add
 SILU = mybir.ActivationFunctionType.Silu
+COPY = mybir.ActivationFunctionType.Copy
 
 P = 128
 K = 512
 T = 2048
 S = 1024
 PACK = 4
+LAST = PACK - 1
 CH = 256
 NCH = S // CH
 BANK = 512
+BLOCKS = BANK // P
 FLOPS = 2 * 2 * K * K * S
 
 
@@ -32,12 +35,11 @@ def tile_moe_mod_silu_kernel(
     with ExitStack() as ctx:
         keep = ctx.enter_context(tc.tile_pool(name="keep", bufs=1))
         ring = ctx.enter_context(tc.tile_pool(name="ring", bufs=3))
-        mm_ps = ctx.enter_context(tc.psum_pool(name="mm_ps", bufs=2))
-        a_ps = ctx.enter_context(tc.psum_pool(name="a_ps", bufs=3))
-        b_ps = ctx.enter_context(tc.psum_pool(name="b_ps", bufs=3))
+        mm_ps = ctx.enter_context(tc.psum_pool(name="mm_ps", bufs=4))
+        turn_ps = ctx.enter_context(tc.psum_pool(name="turn_ps", bufs=1))
 
-        def held(name, shape, dtype):
-            return keep.tile(shape, dtype, name=name, align_bytes=64)
+        def held(name, shape, dtype, tag=None):
+            return keep.tile(shape, dtype, name=name, tag=tag or name, align_bytes=64)
 
         idx1 = keep.tile([P, S // 16], U16, name="idx1")
         idx2 = keep.tile([P, S // 16], U16, name="idx2")
@@ -49,152 +51,181 @@ def tile_moe_mod_silu_kernel(
         w1_s = held("w1_s", [P, K], U8)
         w2_raw = held("w2_raw", [P, K], I32)
         w2s_raw = held("w2s_raw", [P, K], U8)
-        w2_q = held("w2_q", [P, K], I32)
-        w2_s = held("w2_s", [P, K], U8)
         g1 = held("g1", [P, S], F32)
         g2 = held("g2", [P, S], F32)
         ident = held("ident", [P, P], F32)
         warm = held("warm", [P, 8], F32)
         res = [held(f"res{t}", [P, T], F32) for t in range(PACK)]
-        r = [held(f"r{t}", [P, T], F32) for t in range(PACK)]
-        spread = [held(f"spread{i}", [P, T], F32) for i in range(2)]
+        r_turned = [held(f"r_turned{t}", [P, T], F32) for t in range(LAST)]
+        r16 = [held(f"r16_{t}", [P, T], BF16) for t in range(LAST)]
+        spread1 = [held(f"spread1_{i}", [P, T], F32) for i in range(2)]
         gw = [held(f"gw{c}", [P, CH], U32) for c in range(NCH)]
         gs = [held(f"gs{c}", [P, CH], U8) for c in range(NCH)]
-        y = [held(f"y{t}", [P, S], F32) for t in range(PACK)]
-        z = [held(f"z{t}", [P, S], F32) for t in range(PACK)]
-        rg = [held(f"rg{c}", [P, PACK, CH], F32) for c in range(NCH)]
-        rb = [held(f"rb{c}", [P, CH * PACK], BF16) for c in range(NCH)]
+        y = held("y", [P, PACK, S], F32)
+        z = held("z", [P, PACK, S], F32)
+        rb = held("rb", [P, S * PACK], BF16)
         rq = [held(f"rq{c}", [P, CH], U32) for c in range(NCH)]
         rs = [held(f"rs{c}", [P, CH], U8) for c in range(NCH)]
 
         xr_v = xr.rearrange("(p t) c -> p t c", t=PACK)
         out_v = out.rearrange("(p t) c -> p t c", t=PACK)
         w1_v = w1.rearrange("(p j) n -> p j n", j=PACK)
+        rb_v = rb[:].rearrange("p (c t) -> p c t", t=PACK)
+
+        def cols(c, n=1):
+            return slice(c * CH, (c + n) * CH)
+
+        def entries(idx, c, n=1):
+            return idx[:, c * CH // 16 : (c + n) * CH // 16]
+
+        def load_scale_rows(plane, rows):
+            for q in range(4):
+                nc.sync.dma_start(plane[32 * q : 32 * q + 4, :].bitcast(I32), rows[0, 4 * q : 4 * q + 4, :].bitcast(I32))
 
         nc.vector.memset(xs[:].bitcast(I32), 0)
         nc.sync.dma_start(idx1[:], offs)
-        nc.sync.dma_start(xw[:], x_words[0].rearrange("p c d -> p (c d)").bitcast(I32))
-        for q in range(4):
-            nc.scalar.dma_start(xs[32 * q : 32 * q + 4, :].bitcast(I32), x_scales[0, 4 * q : 4 * q + 4, :].bitcast(I32))
+        load_scale_rows(xs, x_scales)
         nc.vector.memset(warm[:], 0.0)
         nc.scalar.activation(warm[:, 4:8], warm[:, 0:4], SILU)
         for h in range(2):
-            nc.sync.dma_start(w1_raw[:, :, h * 256 : (h + 1) * 256], w1_v[:, :, h * 256 : (h + 1) * 256])
-        nc.sync.dma_start(g1[:], gate1)
-        nc.vector.memset(spread[0][:], 0.0)
-        nc.vector.memset(spread[1][:], 0.0)
+            nc.sync.dma_start(w1_raw[:, :, cols(h)], w1_v[:, :, cols(h)])
+        nc.sync.dma_start(xw[:], x_words[0].rearrange("p c d -> p (c d)").bitcast(I32))
+        for h in range(2):
+            nc.sync.dma_start(g1[:, cols(2 * h, 2)], gate1[:, cols(2 * h, 2)])
         nc.vector.memset(w2s_raw[:].bitcast(I32), 0)
+        nc.vector.memset(spread1[0][:], 0.0)
         make_identity(nc, ident[:])
+        nc.gpsimd.memset(spread1[1][:], 0.0)
         for t in range(PACK):
             nc.sync.dma_start(res[t][:], xr_v[:, t, :])
-        nc.sync.dma_start(idx2[:], offs2)
+            if t == 1:
+                nc.sync.dma_start(idx2[:], offs2)
         nc.sync.dma_start(w2_raw[:], w2_words[0].rearrange("p n d -> p (n d)").bitcast(I32))
-        for q in range(4):
-            nc.sync.dma_start(w2s_raw[32 * q : 32 * q + 4, :].bitcast(I32), w2_scales[0, 4 * q : 4 * q + 4, :].bitcast(I32))
+        load_scale_rows(w2s_raw, w2_scales)
         nc.sync.dma_start(g2[:], gate2)
 
-        def cols(c):
-            return slice(c * CH, (c + 1) * CH)
-
-        def entries(idx, c):
-            return idx[:, c * CH // 16 : (c + 1) * CH // 16]
-
+        for c in range(NCH):
+            nc.vector.tensor_copy(gs[c][:], xs[:].indirect(entries(idx1, c)))
         w1_dst = w1_bf[:].rearrange("p (t m j) -> p m t j", t=PACK, j=PACK)
         w1_src = w1_raw[:].rearrange("p j (m t) -> p m t j", t=PACK)
-        for h in range(2):
-            nc.scalar.copy(w1_dst[:, h * 64 : (h + 1) * 64], w1_src[:, h * 64 : (h + 1) * 64])
+        nc.scalar.copy(w1_dst[:, 0:64], w1_src[:, 0:64])
+        nc.vector.tensor_copy(w1_dst[:, 64:128], w1_src[:, 64:128])
+        nc.vector.quantize_mx(out=w1_q[:].bitcast(FP8X4), scales=w1_s[:], in_=w1_bf[:])
 
-        def gather_tokens(c):
-            nc.vector.tensor_copy(gw[c][:], xw[:].bitcast(U32).indirect(entries(idx1, c)))
-            nc.vector.tensor_copy(gs[c][:], xs[:].indirect(entries(idx1, c)))
-
-        def product(wq, ws, codes, scales, dst, t, c0):
-            acc = mm_ps.tile([P, BANK], F32, name="acc")
+        def products(wq, ws, codes, scales, dst, c, t0):
+            acc = mm_ps.tile([P, 2, CH], F32, name="acc")
             for u in range(2):
+                w_cols = slice((t0 + u) * P, (t0 + u + 1) * P)
                 nc.tensor.matmul_mx(
-                    out=acc[:, u * CH : (u + 1) * CH],
-                    lhsT=wq[:, t * P : (t + 1) * P].bitcast(FP8X4),
-                    lhsT_scale=ws[:, t * P : (t + 1) * P],
-                    rhs=codes[c0 + u][:].bitcast(FP8X4),
-                    rhs_scale=scales[c0 + u][:],
+                    out=acc[:, u, :],
+                    lhsT=wq[:, w_cols].bitcast(FP8X4),
+                    lhsT_scale=ws[:, w_cols],
+                    rhs=codes[c][:].bitcast(FP8X4),
+                    rhs_scale=scales[c][:],
                     start=True,
                     stop=True,
                 )
-            nc.scalar.activation(dst[:, c0 * CH : (c0 + 2) * CH], acc[:], SILU)
+            nc.scalar.activation(dst[:, t0 : t0 + 2, cols(c)], acc[:], SILU)
 
-        for c in range(3):
-            gather_tokens(c)
-        nc.vector.quantize_mx(out=w1_q[:].bitcast(FP8X4), scales=w1_s[:], in_=w1_bf[:])
-        gather_tokens(3)
+        for c in range(NCH):
+            nc.vector.tensor_copy(gw[c][:], xw[:].bitcast(U32).indirect(entries(idx1, c)))
+            products(w1_q, w1_s, gw, gs, y, c, 0)
+        for c in range(NCH):
+            products(w1_q, w1_s, gw, gs, y, c, 2)
+
+        def turn(bank, *sources):
+            steps = [(src, b) for src in sources for b in range(BLOCKS)]
+            for i, (src, b) in enumerate(steps):
+                blk = slice(b * P, (b + 1) * P)
+                nc.tensor.matmul(
+                    bank[:, blk], src[:, blk], ident[:], start=i == 0, stop=i == len(steps) - 1, is_transpose=True
+                )
+
+        def scatter(window, idx, values, gate, t, c, n):
+            nc.vector.tensor_tensor(window[:].indirect(entries(idx, c, n)), values[:, t, cols(c, n)], gate[:, cols(c, n)], MULT)
+
+        def gather16(t, c, n):
+            nc.scalar.activation(rb_v[:, cols(c, n), t], r16[t][:].indirect(entries(idx2, c, n)), COPY)
+
+        order = (("there", 0), ("there", 1), ("there", 2), ("back", 0), ("there", 3), ("back", 1), ("back", 2), ("back", 3))
+
+        def sum_by_transposes(there, back):
+            for i, (way, g) in enumerate(order):
+                bank = turn_ps.tile([P, BANK], F32, name=f"bank{i % 4}")
+                (there if way == "there" else back)(bank, g, slice(g * BANK, (g + 1) * BANK))
+
         for t in range(PACK):
-            for c0 in (0, 2):
-                product(w1_q, w1_s, gw, gs, y[t], t, c0)
-
-        def add_by_transposes(t):
-            for g in range(T // BANK):
-                a = a_ps.tile([P, BANK], F32, name="a")
-                for b in range(4):
-                    blk = slice(g * BANK + b * P, g * BANK + (b + 1) * P)
-                    nc.tensor.matmul(a[:, b * P : (b + 1) * P], res[t][:, blk], ident[:], start=True, stop=False, is_transpose=True)
-                    nc.tensor.matmul(a[:, b * P : (b + 1) * P], spread[t % 2][:, blk], ident[:], start=False, stop=True, is_transpose=True)
-                turned = ring.tile([P, BANK], F32, name="turned")
-                nc.scalar.copy(turned[:], a[:])
-                bk = b_ps.tile([P, BANK], F32, name="bk")
-                for b in range(4):
-                    nc.tensor.transpose(bk[:, b * P : (b + 1) * P], turned[:, b * P : (b + 1) * P], ident[:])
-                nc.scalar.copy(r[t][:, g * BANK : (g + 1) * BANK], bk[:])
-
-        def gather_r(t, c):
-            nc.vector.tensor_copy(rg[c][:, t, :], r[t][:].indirect(entries(idx2, c)))
-
-        for t in range(PACK):
+            window = spread1[t % 2]
             if t == 0:
-                for h in range(2):
-                    half = slice(h * 512, (h + 1) * 512)
-                    nc.vector.tensor_tensor(spread[0][:].indirect(idx1[:, h * 32 : (h + 1) * 32]), y[0][:, half], g1[:, half], MULT)
+                for c in range(NCH):
+                    scatter(window, idx1, y, g1, t, c, 1)
             else:
-                nc.vector.tensor_tensor(spread[t % 2][:].indirect(idx1[:]), y[t][:], g1[:], MULT)
-            add_by_transposes(t)
+                scatter(window, idx1, y, g1, t, 0, NCH)
+            if t < LAST:
 
+                def there1(bank, g, span, t=t, window=window):
+                    turn(bank, res[t][:, span], window[:, span])
+                    nc.scalar.copy(r_turned[t][:, span], bank[:])
+
+                def back1(bank, g, span, t=t):
+                    turn(bank, r_turned[t][:, span])
+                    nc.scalar.copy(r16[t][:, span], bank[:])
+
+                sum_by_transposes(there1, back1)
+            if t < 2:
+                gather16(t, 0, NCH)
+        r_last = held("r_last", [P, T], F32, "spread1_0")
+        nc.vector.tensor_tensor(r_last[:], res[LAST][:], spread1[1][:], ADD)
+
+        spread2 = [held(f"spread2_{i}", [P, T], F32, tag) for i, tag in enumerate(("xw", "res0"))]
+        for tile in spread2:
+            nc.gpsimd.memset(tile[:], 0.0)
+        w2_q = held("w2_q", [P, K], I32, "spread1_1")
+        w2_s = held("w2_s", [P, K], U8, "res3")
+
+        def gather_last(c):
+            rg = ring.tile([P, CH], F32, name="rg", bufs=2)
+            nc.vector.tensor_copy(rg[:], r_last[:].indirect(entries(idx2, c)))
+            return rg
+
+        gathered = [gather_last(0)]
         nc.vector.tensor_copy(w2_q[:].rearrange("p (t m) -> p t m", t=PACK), w2_raw[:].rearrange("p (m t) -> p t m", t=PACK))
         nc.vector.tensor_copy(w2_s[:].rearrange("p (t m) -> p t m", t=PACK), w2s_raw[:].rearrange("p (m t) -> p t m", t=PACK))
-        for c in range(3):
-            for t in range(3):
-                gather_r(t, c)
+        gathered.append(gather_last(1))
+        for c in range(NCH):
+            gather16(2, c, 1)
+            nc.scalar.copy(rb_v[:, cols(c), LAST], gathered[c][:])
+            nc.vector.quantize_mx(
+                out=rq[c][:].bitcast(FP8X4), scales=rs[c][:], in_=rb[:, c * CH * PACK : (c + 1) * CH * PACK]
+            )
+            if c + 2 < NCH:
+                gathered.append(gather_last(c + 2))
+            products(w2_q, w2_s, rq, rs, z, c, 0)
+        for c in range(NCH):
+            products(w2_q, w2_s, rq, rs, z, c, 2)
 
-        def round_r(c):
-            nc.scalar.copy(rb[c][:].rearrange("p (c t) -> p c t", t=PACK), rg[c][:].rearrange("p t c -> p c t"))
+        pieces = {0: [(0, 1), (1, 1), (2, 1), (3, 1)], 1: [(0, 1), (1, 3)], 2: [(0, 4)], 3: [(0, 4)]}
+        for t in range(PACK):
+            window = spread2[t % 2]
+            for c, n in pieces[t]:
+                scatter(window, idx2, z, g2, t, c, n)
+            if t < LAST:
+                turned = {}
 
-        def quant_r(c):
-            nc.vector.quantize_mx(out=rq[c][:].bitcast(FP8X4), scales=rs[c][:], in_=rb[c][:])
+                def there2(bank, g, span, window=window, turned=turned):
+                    turn(bank, window[:, span])
+                    turned[g] = ring.tile([P, BANK], F32, name="turned", bufs=4)
+                    nc.scalar.copy(turned[g][:], bank[:])
 
-        gather_r(3, 0)
-        round_r(0)
-        gather_r(3, 1)
-        round_r(1)
-        gather_r(3, 2)
-        round_r(2)
-        for t in range(PACK):
-            gather_r(t, 3)
-            if t == 1:
-                quant_r(0)
-            if t == 3:
-                quant_r(1)
-        round_r(3)
-        for t in range(PACK):
-            product(w2_q, w2_s, rq, rs, z[t], t, 0)
-        quant_r(2)
-        quant_r(3)
-        for t in range(PACK):
-            product(w2_q, w2_s, rq, rs, z[t], t, 2)
+                def back2(bank, g, span, t=t, turned=turned):
+                    turn(bank, r_turned[t][:, span], turned[g][:])
+                    done = ring.tile([P, BANK], F32, name="done", bufs=4)
+                    nc.scalar.copy(done[:], bank[:])
+                    nc.sync.dma_start(out_v[:, t, span], done[:])
 
-        for t in range(PACK):
-            for h in range(2):
-                half = slice(h * 512, (h + 1) * 512)
-                u = ring.tile([P, 512], F32, name="u")
-                v = ring.tile([P, 512], F32, name="v")
-                nc.vector.tensor_tensor(u[:], z[t][:, half], g2[:, half], MULT)
-                for e in range(2):
-                    nc.vector.tensor_tensor(v[:, e * CH : (e + 1) * CH], u[:, e * CH : (e + 1) * CH], rg[2 * h + e][:, t, :], ADD)
-                nc.vector.tensor_copy(r[t][:].indirect(idx2[:, h * 32 : (h + 1) * 32]), v[:])
-            nc.sync.dma_start(out_v[:, t, :], r[t][:])
+                sum_by_transposes(there2, back2)
+        done_last = held("done_last", [P, T], F32, "r_turned2")
+        for g in range(T // BANK):
+            span = slice(g * BANK, (g + 1) * BANK)
+            nc.vector.tensor_tensor(done_last[:, span], r_last[:, span], spread2[1][:, span], ADD)
+            nc.sync.dma_start(out_v[:, LAST, span], done_last[:, span])

@@ -25,6 +25,8 @@ CH = 256
 NCH = S // CH
 BANK = 512
 BLOCKS = BANK // P
+ORDER1 = (2, 0, 1, 3)
+PIECES = ((0, 1), (1, 1), (2, 2))
 FLOPS = 2 * 2 * K * K * S
 
 
@@ -35,7 +37,7 @@ def tile_moe_mod_silu_kernel(
     with ExitStack() as ctx:
         keep = ctx.enter_context(tc.tile_pool(name="keep", bufs=1))
         ring = ctx.enter_context(tc.tile_pool(name="ring", bufs=3))
-        mm_ps = ctx.enter_context(tc.psum_pool(name="mm_ps", bufs=4))
+        mm_ps = ctx.enter_context(tc.psum_pool(name="mm_ps", bufs=2))
         turn_ps = ctx.enter_context(tc.psum_pool(name="turn_ps", bufs=1))
 
         def held(name, shape, dtype, tag=None):
@@ -56,16 +58,16 @@ def tile_moe_mod_silu_kernel(
         ident = held("ident", [P, P], F32)
         warm = held("warm", [P, 8], F32)
         res = [held(f"res{t}", [P, T], F32) for t in range(PACK)]
-        r_turned = [held(f"r_turned{t}", [P, T], F32) for t in range(LAST)]
-        r16 = [held(f"r16_{t}", [P, T], BF16) for t in range(LAST)]
+        r_turned = {}
+        r16 = {}
         spread1 = [held(f"spread1_{i}", [P, T], F32) for i in range(2)]
-        gw = [held(f"gw{c}", [P, CH], U32) for c in range(NCH)]
-        gs = [held(f"gs{c}", [P, CH], U8) for c in range(NCH)]
+        gw = held("gw", [P, S], U32)
+        gs = held("gs", [P, S], U8)
         y = held("y", [P, PACK, S], F32)
         z = held("z", [P, PACK, S], F32)
         rb = held("rb", [P, S * PACK], BF16)
-        rq = [held(f"rq{c}", [P, CH], U32) for c in range(NCH)]
-        rs = [held(f"rs{c}", [P, CH], U8) for c in range(NCH)]
+        rq = held("rq", [P, S], U32)
+        rs = held("rs", [P, S], U8)
 
         xr_v = xr.rearrange("(p t) c -> p t c", t=PACK)
         out_v = out.rearrange("(p t) c -> p t c", t=PACK)
@@ -82,7 +84,7 @@ def tile_moe_mod_silu_kernel(
             for q in range(4):
                 nc.sync.dma_start(plane[32 * q : 32 * q + 4, :].bitcast(I32), rows[0, 4 * q : 4 * q + 4, :].bitcast(I32))
 
-        nc.vector.memset(xs[:].bitcast(I32), 0)
+        nc.gpsimd.memset(xs[:].bitcast(I32), 0)
         nc.sync.dma_start(idx1[:], offs)
         load_scale_rows(xs, x_scales)
         nc.vector.memset(warm[:], 0.0)
@@ -96,16 +98,18 @@ def tile_moe_mod_silu_kernel(
         nc.vector.memset(spread1[0][:], 0.0)
         make_identity(nc, ident[:])
         nc.gpsimd.memset(spread1[1][:], 0.0)
-        for t in range(PACK):
+        zeros = warm[:, 0:1].to_broadcast([P, T])
+        spread2 = [held("spread2_0", [P, T], F32)]
+        nc.scalar.copy(spread2[0][:], zeros)
+        for n, t in enumerate(ORDER1):
             nc.sync.dma_start(res[t][:], xr_v[:, t, :])
-            if t == 1:
+            if n == 1:
                 nc.sync.dma_start(idx2[:], offs2)
         nc.sync.dma_start(w2_raw[:], w2_words[0].rearrange("p n d -> p (n d)").bitcast(I32))
         load_scale_rows(w2s_raw, w2_scales)
         nc.sync.dma_start(g2[:], gate2)
 
-        for c in range(NCH):
-            nc.vector.tensor_copy(gs[c][:], xs[:].indirect(entries(idx1, c)))
+        nc.vector.tensor_copy(gs[:], xs[:].indirect(idx1[:]))
         w1_dst = w1_bf[:].rearrange("p (t m j) -> p m t j", t=PACK, j=PACK)
         w1_src = w1_raw[:].rearrange("p j (m t) -> p m t j", t=PACK)
         nc.scalar.copy(w1_dst[:, 0:64], w1_src[:, 0:64])
@@ -120,18 +124,20 @@ def tile_moe_mod_silu_kernel(
                     out=acc[:, u, :],
                     lhsT=wq[:, w_cols].bitcast(FP8X4),
                     lhsT_scale=ws[:, w_cols],
-                    rhs=codes[c][:].bitcast(FP8X4),
-                    rhs_scale=scales[c][:],
+                    rhs=codes[:, cols(c)].bitcast(FP8X4),
+                    rhs_scale=scales[:, cols(c)],
                     start=True,
                     stop=True,
                 )
             nc.scalar.activation(dst[:, t0 : t0 + 2, cols(c)], acc[:], SILU)
 
-        for c in range(NCH):
-            nc.vector.tensor_copy(gw[c][:], xw[:].bitcast(U32).indirect(entries(idx1, c)))
-            products(w1_q, w1_s, gw, gs, y, c, 0)
-        for c in range(NCH):
-            products(w1_q, w1_s, gw, gs, y, c, 2)
+        for c, n in PIECES:
+            nc.vector.tensor_copy(gw[:, cols(c, n)], xw[:].bitcast(U32).indirect(entries(idx1, c, n)))
+        for t0 in (2, 0):
+            for c in range(NCH):
+                products(w1_q, w1_s, gw, gs, y, c, t0)
+        spread2.append(held("spread2_1", [P, T], F32, "gw"))
+        nc.scalar.copy(spread2[1][:], zeros)
 
         def turn(bank, *sources):
             steps = [(src, b) for src in sources for b in range(BLOCKS)]
@@ -147,21 +153,22 @@ def tile_moe_mod_silu_kernel(
         def gather16(t, c, n):
             nc.scalar.activation(rb_v[:, cols(c, n), t], r16[t][:].indirect(entries(idx2, c, n)), COPY)
 
-        order = (("there", 0), ("there", 1), ("there", 2), ("back", 0), ("there", 3), ("back", 1), ("back", 2), ("back", 3))
+        def sum_by_transposes(n, there, back):
+            for i in range(8):
+                g = i % 4
+                bank = turn_ps.tile([P, BANK], F32, name=f"bank{(3 * n + i) % 6}")
+                (there if i < 4 else back)(bank, g, slice(g * BANK, (g + 1) * BANK))
 
-        def sum_by_transposes(there, back):
-            for i, (way, g) in enumerate(order):
-                bank = turn_ps.tile([P, BANK], F32, name=f"bank{i % 4}")
-                (there if way == "there" else back)(bank, g, slice(g * BANK, (g + 1) * BANK))
-
-        for t in range(PACK):
-            window = spread1[t % 2]
-            if t == 0:
-                for c in range(NCH):
-                    scatter(window, idx1, y, g1, t, c, 1)
+        for n, t in enumerate(ORDER1):
+            window = spread1[n % 2]
+            if n == 0:
+                for c, m in PIECES:
+                    scatter(window, idx1, y, g1, t, c, m)
             else:
                 scatter(window, idx1, y, g1, t, 0, NCH)
             if t < LAST:
+                r_turned[t] = held(f"r_turned{t}", [P, T], F32, f"r16_{ORDER1[n - 1]}" if n else None)
+                r16[t] = held(f"r16_{t}", [P, T], BF16)
 
                 def there1(bank, g, span, t=t, window=window):
                     turn(bank, res[t][:, span], window[:, span])
@@ -171,40 +178,30 @@ def tile_moe_mod_silu_kernel(
                     turn(bank, r_turned[t][:, span])
                     nc.scalar.copy(r16[t][:, span], bank[:])
 
-                sum_by_transposes(there1, back1)
-            if t < 2:
+                sum_by_transposes(n, there1, back1)
+            if n < 2:
                 gather16(t, 0, NCH)
         r_last = held("r_last", [P, T], F32, "spread1_0")
         nc.vector.tensor_tensor(r_last[:], res[LAST][:], spread1[1][:], ADD)
 
-        spread2 = [held(f"spread2_{i}", [P, T], F32, tag) for i, tag in enumerate(("xw", "res0"))]
-        for tile in spread2:
-            nc.gpsimd.memset(tile[:], 0.0)
         w2_q = held("w2_q", [P, K], I32, "spread1_1")
         w2_s = held("w2_s", [P, K], U8, "res3")
 
-        def gather_last(c):
-            rg = ring.tile([P, CH], F32, name="rg", bufs=2)
-            nc.vector.tensor_copy(rg[:], r_last[:].indirect(entries(idx2, c)))
-            return rg
-
-        gathered = [gather_last(0)]
+        nc.vector.tensor_copy(rb_v[:, :, LAST], r_last[:].indirect(idx2[:]))
         nc.vector.tensor_copy(w2_q[:].rearrange("p (t m) -> p t m", t=PACK), w2_raw[:].rearrange("p (m t) -> p t m", t=PACK))
         nc.vector.tensor_copy(w2_s[:].rearrange("p (t m) -> p t m", t=PACK), w2s_raw[:].rearrange("p (m t) -> p t m", t=PACK))
-        gathered.append(gather_last(1))
         for c in range(NCH):
-            gather16(2, c, 1)
-            nc.scalar.copy(rb_v[:, cols(c), LAST], gathered[c][:])
+            gather16(ORDER1[2], c, 1)
             nc.vector.quantize_mx(
-                out=rq[c][:].bitcast(FP8X4), scales=rs[c][:], in_=rb[:, c * CH * PACK : (c + 1) * CH * PACK]
+                out=rq[:, cols(c)].bitcast(FP8X4),
+                scales=rs[:, cols(c)],
+                in_=rb[:, c * CH * PACK : (c + 1) * CH * PACK],
             )
-            if c + 2 < NCH:
-                gathered.append(gather_last(c + 2))
             products(w2_q, w2_s, rq, rs, z, c, 0)
         for c in range(NCH):
             products(w2_q, w2_s, rq, rs, z, c, 2)
 
-        pieces = {0: [(0, 1), (1, 1), (2, 1), (3, 1)], 1: [(0, 1), (1, 3)], 2: [(0, 4)], 3: [(0, 4)]}
+        pieces = {0: [(0, 1), (1, 1), (2, 1), (3, 1)], 1: [(0, 4)], 2: [(0, 4)], 3: [(0, 4)]}
         for t in range(PACK):
             window = spread2[t % 2]
             for c, n in pieces[t]:
@@ -223,9 +220,10 @@ def tile_moe_mod_silu_kernel(
                     nc.scalar.copy(done[:], bank[:])
                     nc.sync.dma_start(out_v[:, t, span], done[:])
 
-                sum_by_transposes(there2, back2)
+                sum_by_transposes(LAST + t, there2, back2)
         done_last = held("done_last", [P, T], F32, "r_turned2")
-        for g in range(T // BANK):
-            span = slice(g * BANK, (g + 1) * BANK)
+        edges = (0, 256, 768, 1280, 1792, 2048)
+        for lo, hi in zip(edges, edges[1:]):
+            span = slice(lo, hi)
             nc.vector.tensor_tensor(done_last[:, span], r_last[:, span], spread2[1][:, span], ADD)
             nc.sync.dma_start(out_v[:, LAST, span], done_last[:, span])

@@ -116,9 +116,9 @@ def tile_moe_mod_silu_kernel(
         nc.vector.tensor_copy(w1_dst[:, 64:128], w1_src[:, 64:128])
         nc.vector.quantize_mx(out=w1_q[:].bitcast(FP8X4), scales=w1_s[:], in_=w1_bf[:])
 
-        def products(wq, ws, codes, scales, dst, c, t0):
-            acc = mm_ps.tile([P, 2, CH], F32, name="acc")
-            for u in range(2):
+        def products(wq, ws, codes, scales, dst, c, t0, planes=2):
+            acc = mm_ps.tile([P, planes, CH], F32, name="acc")
+            for u in range(planes):
                 w_cols = slice((t0 + u) * P, (t0 + u + 1) * P)
                 nc.tensor.matmul_mx(
                     out=acc[:, u, :],
@@ -129,7 +129,7 @@ def tile_moe_mod_silu_kernel(
                     start=True,
                     stop=True,
                 )
-            nc.scalar.activation(dst[:, t0 : t0 + 2, cols(c)], acc[:], SILU)
+            nc.scalar.activation(dst[:, t0 : t0 + planes, cols(c)], acc[:], SILU)
 
         for c, n in PIECES:
             nc.vector.tensor_copy(gw[:, cols(c, n)], xw[:].bitcast(U32).indirect(entries(idx1, c, n)))
@@ -162,7 +162,7 @@ def tile_moe_mod_silu_kernel(
         for n, t in enumerate(ORDER1):
             window = spread1[n % 2]
             if n == 0:
-                for c, m in PIECES:
+                for c, m in ((0, 2), (2, 2)):
                     scatter(window, idx1, y, g1, t, c, m)
             else:
                 scatter(window, idx1, y, g1, t, 0, NCH)
@@ -181,14 +181,14 @@ def tile_moe_mod_silu_kernel(
                 sum_by_transposes(n, there1, back1)
             if n < 2:
                 gather16(t, 0, NCH)
+        w2_q = held("w2_q", [P, K], I32, "res1")
+        nc.vector.tensor_copy(w2_q[:].rearrange("p (t m) -> p t m", t=PACK), w2_raw[:].rearrange("p (m t) -> p t m", t=PACK))
         r_last = held("r_last", [P, T], F32, "spread1_0")
         nc.vector.tensor_tensor(r_last[:], res[LAST][:], spread1[1][:], ADD)
 
-        w2_q = held("w2_q", [P, K], I32, "spread1_1")
         w2_s = held("w2_s", [P, K], U8, "res3")
 
         nc.vector.tensor_copy(rb_v[:, :, LAST], r_last[:].indirect(idx2[:]))
-        nc.vector.tensor_copy(w2_q[:].rearrange("p (t m) -> p t m", t=PACK), w2_raw[:].rearrange("p (m t) -> p t m", t=PACK))
         nc.vector.tensor_copy(w2_s[:].rearrange("p (t m) -> p t m", t=PACK), w2s_raw[:].rearrange("p (m t) -> p t m", t=PACK))
         for c in range(NCH):
             gather16(ORDER1[2], c, 1)
@@ -197,14 +197,20 @@ def tile_moe_mod_silu_kernel(
                 scales=rs[:, cols(c)],
                 in_=rb[:, c * CH * PACK : (c + 1) * CH * PACK],
             )
-            products(w2_q, w2_s, rq, rs, z, c, 0)
+            if c == 0:
+                products(w2_q, w2_s, rq, rs, z, 0, 0, 1)
+                products(w2_q, w2_s, rq, rs, z, 0, 1, 1)
+            else:
+                products(w2_q, w2_s, rq, rs, z, c, 0)
         for c in range(NCH):
             products(w2_q, w2_s, rq, rs, z, c, 2)
 
-        pieces = {0: [(0, 1), (1, 1), (2, 1), (3, 1)], 1: [(0, 4)], 2: [(0, 4)], 3: [(0, 4)]}
+        for t in range(2):
+            scatter(spread2[t], idx2, z, g2, t, 0, 1)
+        rest = (((1, 1), (2, 2)), ((1, 3),), ((0, 4),), ((0, 4),))
         for t in range(PACK):
             window = spread2[t % 2]
-            for c, n in pieces[t]:
+            for c, n in rest[t]:
                 scatter(window, idx2, z, g2, t, c, n)
             if t < LAST:
                 turned = {}

@@ -1,7 +1,6 @@
 from contextlib import ExitStack
 
 import concourse.mybir as mybir
-from concourse.masks import make_identity
 
 F32 = mybir.dt.float32
 BF16 = mybir.dt.bfloat16
@@ -20,13 +19,10 @@ K = 512
 T = 2048
 S = 1024
 PACK = 4
-LAST = PACK - 1
 CH = 256
 NCH = S // CH
 BANK = 512
-BLOCKS = BANK // P
-ORDER1 = (2, 0, 1, 3)
-PIECES = ((0, 1), (1, 1), (2, 2))
+A, B, C, L = 2, 1, 0, 3
 FLOPS = 2 * 2 * K * K * S
 
 
@@ -36,9 +32,7 @@ def tile_moe_mod_silu_kernel(
     nc = tc.nc
     with ExitStack() as ctx:
         keep = ctx.enter_context(tc.tile_pool(name="keep", bufs=1))
-        ring = ctx.enter_context(tc.tile_pool(name="ring", bufs=3))
-        mm_ps = ctx.enter_context(tc.psum_pool(name="mm_ps", bufs=2))
-        turn_ps = ctx.enter_context(tc.psum_pool(name="turn_ps", bufs=1))
+        mm_ps = ctx.enter_context(tc.psum_pool(name="mm_ps", bufs=6))
 
         def held(name, shape, dtype, tag=None):
             return keep.tile(shape, dtype, name=name, tag=tag or name, align_bytes=64)
@@ -47,24 +41,21 @@ def tile_moe_mod_silu_kernel(
         idx2 = keep.tile([P, S // 16], U16, name="idx2")
         xw = held("xw", [P, T], I32)
         xs = held("xs", [P, T], U8)
-        w1_raw = held("w1_raw", [P, PACK, K], F32)
-        w1_bf = held("w1_bf", [P, K * PACK], BF16)
+        w1_raw = [held(f"w1_raw{h}", [P, PACK, K // 2], F32) for h in range(2)]
+        w1_bf = held("w1_bf", [P, 2 * K], BF16)
         w1_q = held("w1_q", [P, K], U32)
         w1_s = held("w1_s", [P, K], U8)
         w2_raw = held("w2_raw", [P, K], I32)
         w2s_raw = held("w2s_raw", [P, K], U8)
         g1 = held("g1", [P, S], F32)
         g2 = held("g2", [P, S], F32)
-        ident = held("ident", [P, P], F32)
         warm = held("warm", [P, 8], F32)
         res = [held(f"res{t}", [P, T], F32) for t in range(PACK)]
-        r_turned = {}
-        r16 = {}
-        spread1 = [held(f"spread1_{i}", [P, T], F32) for i in range(2)]
+        spread1 = [held(f"spread1_{i}", [P, T], F32) for i in range(3)]
         gw = held("gw", [P, S], U32)
         gs = held("gs", [P, S], U8)
-        y = held("y", [P, PACK, S], F32)
-        z = held("z", [P, PACK, S], F32)
+        y = [held(f"y{t}", [P, S], F32) for t in range(PACK)]
+        z = [held(f"z{t}", [P, S], F32) for t in range(PACK)]
         rb = held("rb", [P, S * PACK], BF16)
         rq = held("rq", [P, S], U32)
         rs = held("rs", [P, S], U8)
@@ -84,152 +75,122 @@ def tile_moe_mod_silu_kernel(
             for q in range(4):
                 nc.sync.dma_start(plane[32 * q : 32 * q + 4, :].bitcast(I32), rows[0, 4 * q : 4 * q + 4, :].bitcast(I32))
 
-        nc.gpsimd.memset(xs[:].bitcast(I32), 0)
+        nc.gpsimd.memset(xs[:, : T // 2].bitcast(I32), 0)
+        nc.vector.memset(xs[:, T // 2 :].bitcast(I32), 0)
+        nc.gpsimd.memset(w2s_raw[:].bitcast(I32), 0)
         nc.sync.dma_start(idx1[:], offs)
+        nc.sync.dma_start(idx2[:], offs2)
         load_scale_rows(xs, x_scales)
         nc.vector.memset(warm[:], 0.0)
         nc.scalar.activation(warm[:, 4:8], warm[:, 0:4], SILU)
-        for h in range(2):
-            nc.sync.dma_start(w1_raw[:, :, cols(h)], w1_v[:, :, cols(h)])
         nc.sync.dma_start(xw[:], x_words[0].rearrange("p c d -> p (c d)").bitcast(I32))
         for h in range(2):
-            nc.sync.dma_start(g1[:, cols(2 * h, 2)], gate1[:, cols(2 * h, 2)])
-        nc.vector.memset(w2s_raw[:].bitcast(I32), 0)
-        nc.vector.memset(spread1[0][:], 0.0)
-        make_identity(nc, ident[:])
+            nc.sync.dma_start(w1_raw[h][:], w1_v[:, :, cols(h)])
+        nc.sync.dma_start(g1[:, cols(0)], gate1[:, cols(0)])
+        load_scale_rows(w2s_raw, w2_scales)
+        nc.sync.dma_start(w2_raw[:], w2_words[0].rearrange("p n d -> p (n d)").bitcast(I32))
+        nc.sync.dma_start(g1[:, cols(1, 3)], gate1[:, cols(1, 3)])
+        nc.gpsimd.memset(spread1[0][:], 0.0)
         nc.gpsimd.memset(spread1[1][:], 0.0)
+        nc.gpsimd.memset(spread1[2][:], 0.0)
         zeros = warm[:, 0:1].to_broadcast([P, T])
         spread2 = [held("spread2_0", [P, T], F32)]
         nc.scalar.copy(spread2[0][:], zeros)
-        for n, t in enumerate(ORDER1):
+        for t in (A, B, C, L):
             nc.sync.dma_start(res[t][:], xr_v[:, t, :])
-            if n == 1:
-                nc.sync.dma_start(idx2[:], offs2)
-        nc.sync.dma_start(w2_raw[:], w2_words[0].rearrange("p n d -> p (n d)").bitcast(I32))
-        load_scale_rows(w2s_raw, w2_scales)
         nc.sync.dma_start(g2[:], gate2)
 
         nc.vector.tensor_copy(gs[:], xs[:].indirect(idx1[:]))
-        w1_dst = w1_bf[:].rearrange("p (t m j) -> p m t j", t=PACK, j=PACK)
-        w1_src = w1_raw[:].rearrange("p j (m t) -> p m t j", t=PACK)
-        nc.scalar.copy(w1_dst[:, 0:64], w1_src[:, 0:64])
-        nc.vector.tensor_copy(w1_dst[:, 64:128], w1_src[:, 64:128])
-        nc.vector.quantize_mx(out=w1_q[:].bitcast(FP8X4), scales=w1_s[:], in_=w1_bf[:])
-
-        def products(wq, ws, codes, scales, dst, c, t0, planes=2):
-            acc = mm_ps.tile([P, planes, CH], F32, name="acc")
-            for u in range(planes):
-                w_cols = slice((t0 + u) * P, (t0 + u + 1) * P)
-                nc.tensor.matmul_mx(
-                    out=acc[:, u, :],
-                    lhsT=wq[:, w_cols].bitcast(FP8X4),
-                    lhsT_scale=ws[:, w_cols],
-                    rhs=codes[:, cols(c)].bitcast(FP8X4),
-                    rhs_scale=scales[:, cols(c)],
-                    start=True,
-                    stop=True,
-                )
-            nc.scalar.activation(dst[:, t0 : t0 + planes, cols(c)], acc[:], SILU)
-
-        for c, n in PIECES:
-            nc.vector.tensor_copy(gw[:, cols(c, n)], xw[:].bitcast(U32).indirect(entries(idx1, c, n)))
-        for t0 in (2, 0):
-            for c in range(NCH):
-                products(w1_q, w1_s, gw, gs, y, c, t0)
-        spread2.append(held("spread2_1", [P, T], F32, "gw"))
-        nc.scalar.copy(spread2[1][:], zeros)
-
-        def turn(bank, *sources):
-            steps = [(src, b) for src in sources for b in range(BLOCKS)]
-            for i, (src, b) in enumerate(steps):
-                blk = slice(b * P, (b + 1) * P)
-                nc.tensor.matmul(
-                    bank[:, blk], src[:, blk], ident[:], start=i == 0, stop=i == len(steps) - 1, is_transpose=True
-                )
-
-        def scatter(window, idx, values, gate, t, c, n):
-            nc.vector.tensor_tensor(window[:].indirect(entries(idx, c, n)), values[:, t, cols(c, n)], gate[:, cols(c, n)], MULT)
-
-        def gather16(t, c, n):
-            nc.scalar.activation(rb_v[:, cols(c, n), t], r16[t][:].indirect(entries(idx2, c, n)), COPY)
-
-        def sum_by_transposes(n, there, back):
-            for i in range(8):
-                g = i % 4
-                bank = turn_ps.tile([P, BANK], F32, name=f"bank{(3 * n + i) % 6}")
-                (there if i < 4 else back)(bank, g, slice(g * BANK, (g + 1) * BANK))
-
-        for n, t in enumerate(ORDER1):
-            window = spread1[n % 2]
-            if n == 0:
-                for c, m in ((0, 2), (2, 2)):
-                    scatter(window, idx1, y, g1, t, c, m)
-            else:
-                scatter(window, idx1, y, g1, t, 0, NCH)
-            if t < LAST:
-                r_turned[t] = held(f"r_turned{t}", [P, T], F32, f"r16_{ORDER1[n - 1]}" if n else None)
-                r16[t] = held(f"r16_{t}", [P, T], BF16)
-
-                def there1(bank, g, span, t=t, window=window):
-                    turn(bank, res[t][:, span], window[:, span])
-                    nc.scalar.copy(r_turned[t][:, span], bank[:])
-
-                def back1(bank, g, span, t=t):
-                    turn(bank, r_turned[t][:, span])
-                    nc.scalar.copy(r16[t][:, span], bank[:])
-
-                sum_by_transposes(n, there1, back1)
-            if n < 2:
-                gather16(t, 0, NCH)
-        w2_q = held("w2_q", [P, K], I32, "res1")
-        nc.vector.tensor_copy(w2_q[:].rearrange("p (t m) -> p t m", t=PACK), w2_raw[:].rearrange("p (m t) -> p t m", t=PACK))
-        r_last = held("r_last", [P, T], F32, "spread1_0")
-        nc.vector.tensor_tensor(r_last[:], res[LAST][:], spread1[1][:], ADD)
-
-        w2_s = held("w2_s", [P, K], U8, "res3")
-
-        nc.vector.tensor_copy(rb_v[:, :, LAST], r_last[:].indirect(idx2[:]))
+        nc.vector.tensor_copy(gw[:], xw[:].bitcast(U32).indirect(idx1[:]))
+        src = [w1_raw[h][:].rearrange("p j (m t) -> p m t j", t=PACK) for h in range(2)]
+        dst = w1_bf[:].rearrange("p (u m j) -> p m u j", u=2, j=PACK)
+        nc.scalar.copy(dst[:, 0:64], src[0][:, :, 1:3])
+        nc.scalar.copy(dst[:, 64:128, 1], src[1][:, :, 2])
+        nc.vector.tensor_copy(dst[:, 64:128, 0], src[1][:, :, 1])
+        slot1 = {A: 0, B: 1, C: 2, L: 3}
+        for t, u in ((A, 1), (B, 0)):
+            w_cols = slice(slot1[t] * P, (slot1[t] + 1) * P)
+            nc.vector.quantize_mx(out=w1_q[:, w_cols].bitcast(FP8X4), scales=w1_s[:, w_cols], in_=w1_bf[:, u * K : (u + 1) * K])
+        w1_bf2 = held("w1_bf2", [P, 2 * K], BF16, "w1_bf")
+        dst2 = w1_bf2[:].rearrange("p (u m j) -> p m u j", u=2, j=PACK)
+        for h in range(2):
+            nc.vector.tensor_copy(dst2[:, 64 * h : 64 * (h + 1)], src[h][:, :, 0:4:3])
+        nc.vector.quantize_mx(out=w1_q[:, 2 * P :].bitcast(FP8X4), scales=w1_s[:, 2 * P :], in_=w1_bf2[:])
+        w2_q = held("w2_q", [P, K], I32, "w1_bf")
+        w2_s = held("w2_s", [P, K], U8, "w1_raw1")
         nc.vector.tensor_copy(w2_s[:].rearrange("p (t m) -> p t m", t=PACK), w2s_raw[:].rearrange("p (m t) -> p t m", t=PACK))
+        nc.vector.tensor_copy(w2_q[:].rearrange("p (t m) -> p t m", t=PACK), w2_raw[:].rearrange("p (m t) -> p t m", t=PACK))
+
+        def product(wq, ws, slot, codes, scales, dst, c, n):
+            acc = mm_ps.tile([P, n * CH], F32, name="acc")
+            w_cols = slice(slot * P, (slot + 1) * P)
+            nc.tensor.matmul_mx(
+                out=acc[:],
+                lhsT=wq[:, w_cols].bitcast(FP8X4),
+                lhsT_scale=ws[:, w_cols],
+                rhs=codes[:, cols(c, n)].bitcast(FP8X4),
+                rhs_scale=scales[:, cols(c, n)],
+                start=True,
+                stop=True,
+            )
+            nc.scalar.activation(dst[:, cols(c, n)], acc[:], SILU)
+
+        def gated(values, gate, c, n):
+            nc.gpsimd.tensor_tensor(values[:, cols(c, n)], values[:, cols(c, n)], gate[:, cols(c, n)], MULT)
+
+        def scatter(window, idx, values, c, n):
+            nc.vector.tensor_copy(window[:].indirect(entries(idx, c, n)), values[:, cols(c, n)])
+
+        def layer(wq, ws, slot, codes, scales, values, gate, idx, spread):
+            for t, pieces in ((A, ((0, 1),)), (B, ((0, 1),)), (A, ((1, 1), (2, 2))), (B, ((1, 1), (2, 2))), (C, ((0, 2), (2, 2))), (L, ((0, 2), (2, 2)))):
+                for c, n in pieces:
+                    product(wq, ws, slot[t], codes, scales, values[t], c, n)
+                first, count = pieces[0][0], sum(n for c, n in pieces)
+                gated(values[t], gate, first, count)
+                if t != L:
+                    scatter(spread[slot1[t]], idx, values[t], first, count)
+
+        layer(w1_q, w1_s, slot1, gw, gs, y, g1, idx1, spread1)
+        spread2.append(held("spread2_1", [P, T], F32, "gw"))
+        spread2.append(held("spread2_2", [P, T], F32, "w1_q"))
+        nc.scalar.copy(spread2[1][:], zeros)
+        nc.scalar.copy(spread2[2][:], zeros)
+
+        r = {}
+        r16 = {}
+        for t, width in ((A, 1024), (B, 1024), (C, 512)):
+            r[t] = held(f"r{t}", [P, T], F32, f"r16_{A}" if t == C else None)
+            r16[t] = held(f"r16_{t}", [P, T], BF16)
+            for lo in range(0, T, width):
+                span = slice(lo, lo + width)
+                nc.gpsimd.tensor_tensor(r[t][:, span], res[t][:, span], spread1[slot1[t]][:, span], ADD)
+                nc.scalar.copy(r16[t][:, span], r[t][:, span])
+            if t == A:
+                scatter(spread1[0], idx1, y[L], 0, NCH)
+            for c, n in (((0, NCH),) if t != C else tuple((c, 1) for c in range(NCH))):
+                nc.scalar.activation(rb_v[:, cols(c, n), t], r16[t][:].indirect(entries(idx2, c, n)), COPY)
+        r[L] = held("r_last", [P, T], F32, "spread1_2")
+        nc.vector.tensor_tensor(r[L][:], res[L][:], spread1[0][:], ADD)
+
         for c in range(NCH):
-            gather16(ORDER1[2], c, 1)
+            nc.vector.tensor_copy(rb_v[:, cols(c), L], r[L][:].indirect(entries(idx2, c)))
             nc.vector.quantize_mx(
                 out=rq[:, cols(c)].bitcast(FP8X4),
                 scales=rs[:, cols(c)],
                 in_=rb[:, c * CH * PACK : (c + 1) * CH * PACK],
             )
-            if c == 0:
-                products(w2_q, w2_s, rq, rs, z, 0, 0, 1)
-                products(w2_q, w2_s, rq, rs, z, 0, 1, 1)
-            else:
-                products(w2_q, w2_s, rq, rs, z, c, 0)
-        for c in range(NCH):
-            products(w2_q, w2_s, rq, rs, z, c, 2)
-
-        for t in range(2):
-            scatter(spread2[t], idx2, z, g2, t, 0, 1)
-        rest = (((1, 1), (2, 2)), ((1, 3),), ((0, 4),), ((0, 4),))
-        for t in range(PACK):
-            window = spread2[t % 2]
-            for c, n in rest[t]:
-                scatter(window, idx2, z, g2, t, c, n)
-            if t < LAST:
-                turned = {}
-
-                def there2(bank, g, span, window=window, turned=turned):
-                    turn(bank, window[:, span])
-                    turned[g] = ring.tile([P, BANK], F32, name="turned", bufs=4)
-                    nc.scalar.copy(turned[g][:], bank[:])
-
-                def back2(bank, g, span, t=t, turned=turned):
-                    turn(bank, r_turned[t][:, span], turned[g][:])
-                    done = ring.tile([P, BANK], F32, name="done", bufs=4)
-                    nc.scalar.copy(done[:], bank[:])
-                    nc.sync.dma_start(out_v[:, t, span], done[:])
-
-                sum_by_transposes(LAST + t, there2, back2)
-        done_last = held("done_last", [P, T], F32, "r_turned2")
+        layer(w2_q, w2_s, {t: t for t in range(PACK)}, rq, rs, z, g2, idx2, spread2)
+        for t, width, tag in ((A, 1024, f"res{A}"), (B, 1024, f"res{L}"), (C, 512, "xw")):
+            done = held(f"done{t}", [P, T], F32, tag)
+            for lo in range(0, T, width):
+                span = slice(lo, lo + width)
+                nc.gpsimd.tensor_tensor(done[:, span], r[t][:, span], spread2[slot1[t]][:, span], ADD)
+                nc.sync.dma_start(out_v[:, t, span], done[:, span])
+            if t == A:
+                scatter(spread2[0], idx2, z[L], 0, NCH)
+        done_last = held("done_last", [P, T], F32, "w1_q")
         edges = (0, 256, 768, 1280, 1792, 2048)
         for lo, hi in zip(edges, edges[1:]):
             span = slice(lo, hi)
-            nc.vector.tensor_tensor(done_last[:, span], r_last[:, span], spread2[1][:, span], ADD)
-            nc.sync.dma_start(out_v[:, LAST, span], done_last[:, span])
+            nc.vector.tensor_tensor(done_last[:, span], r[L][:, span], spread2[0][:, span], ADD)
+            nc.sync.dma_start(out_v[:, L, span], done_last[:, span])

@@ -1,6 +1,7 @@
 from contextlib import ExitStack
 
 import concourse.mybir as mybir
+from concourse.masks import make_identity
 
 F32 = mybir.dt.float32
 BF16 = mybir.dt.bfloat16
@@ -22,6 +23,8 @@ PACK = 4
 CH = 256
 NCH = S // CH
 BANK = 512
+BLOCKS = BANK // P
+SPANS = T // BANK
 A, B, C, L = 2, 1, 0, 3
 FLOPS = 2 * 2 * K * K * S
 
@@ -32,7 +35,7 @@ def tile_moe_mod_silu_kernel(
     nc = tc.nc
     with ExitStack() as ctx:
         keep = ctx.enter_context(tc.tile_pool(name="keep", bufs=1))
-        mm_ps = ctx.enter_context(tc.psum_pool(name="mm_ps", bufs=6))
+        psum = ctx.enter_context(tc.psum_pool(name="psum", bufs=1))
 
         def held(name, shape, dtype, tag=None):
             return keep.tile(shape, dtype, name=name, tag=tag or name, align_bytes=64)
@@ -42,7 +45,7 @@ def tile_moe_mod_silu_kernel(
         xw = held("xw", [P, T], I32)
         xs = held("xs", [P, T], U8)
         w1_raw = [held(f"w1_raw{h}", [P, PACK, K // 2], F32) for h in range(2)]
-        w1_bf = held("w1_bf", [P, 2 * K], BF16)
+        w1_bf = held("w1_bf", [P, PACK * K], BF16)
         w1_q = held("w1_q", [P, K], U32)
         w1_s = held("w1_s", [P, K], U8)
         w2_raw = held("w2_raw", [P, K], I32)
@@ -51,25 +54,31 @@ def tile_moe_mod_silu_kernel(
         g2 = held("g2", [P, S], F32)
         warm = held("warm", [P, 8], F32)
         res = [held(f"res{t}", [P, T], F32) for t in range(PACK)]
-        spread1 = [held(f"spread1_{i}", [P, T], F32) for i in range(3)]
+        spread1 = [held(f"spread1_{i}", [P, T], F32) for i in range(2)]
+        ident = held("ident", [P, P], F32)
         gw = held("gw", [P, S], U32)
         gs = held("gs", [P, S], U8)
         y = [held(f"y{t}", [P, S], F32) for t in range(PACK)]
         z = [held(f"z{t}", [P, S], F32) for t in range(PACK)]
-        rb = held("rb", [P, S * PACK], BF16)
+        pairs = [held(f"pairs{c}", [P, CH * PACK], BF16) for c in range(1, NCH)]
+        rb = [held(f"rb{c}", [P, CH * PACK], BF16) for c in range(NCH)]
         rq = held("rq", [P, S], U32)
         rs = held("rs", [P, S], U8)
 
         xr_v = xr.rearrange("(p t) c -> p t c", t=PACK)
         out_v = out.rearrange("(p t) c -> p t c", t=PACK)
         w1_v = w1.rearrange("(p j) n -> p j n", j=PACK)
-        rb_v = rb[:].rearrange("p (c t) -> p c t", t=PACK)
 
         def cols(c, n=1):
             return slice(c * CH, (c + n) * CH)
 
         def entries(idx, c, n=1):
             return idx[:, c * CH // 16 : (c + n) * CH // 16]
+
+        def in_pair(c, t):
+            if c == 0:
+                return rb[0][:].rearrange("p (s t) -> p s t", t=PACK)[:, :, t]
+            return pairs[c - 1][:].rearrange("p (u s e) -> p u s e", u=2, e=2)[:, t // 2, :, t % 2]
 
         def load_scale_rows(plane, rows):
             for q in range(4):
@@ -78,54 +87,43 @@ def tile_moe_mod_silu_kernel(
         nc.gpsimd.memset(xs[:, : T // 2].bitcast(I32), 0)
         nc.vector.memset(xs[:, T // 2 :].bitcast(I32), 0)
         nc.gpsimd.memset(w2s_raw[:].bitcast(I32), 0)
+        nc.sync.dma_start(w1_raw[0][:], w1_v[:, :, cols(0)])
         nc.sync.dma_start(idx1[:], offs)
-        nc.sync.dma_start(idx2[:], offs2)
         load_scale_rows(xs, x_scales)
         nc.vector.memset(warm[:], 0.0)
         nc.scalar.activation(warm[:, 4:8], warm[:, 0:4], SILU)
+        nc.sync.dma_start(w1_raw[1][:], w1_v[:, :, cols(1)])
         nc.sync.dma_start(xw[:], x_words[0].rearrange("p c d -> p (c d)").bitcast(I32))
-        for h in range(2):
-            nc.sync.dma_start(w1_raw[h][:], w1_v[:, :, cols(h)])
         nc.sync.dma_start(g1[:, cols(0)], gate1[:, cols(0)])
-        load_scale_rows(w2s_raw, w2_scales)
-        nc.sync.dma_start(w2_raw[:], w2_words[0].rearrange("p n d -> p (n d)").bitcast(I32))
         nc.sync.dma_start(g1[:, cols(1, 3)], gate1[:, cols(1, 3)])
         nc.gpsimd.memset(spread1[0][:], 0.0)
         nc.gpsimd.memset(spread1[1][:], 0.0)
-        nc.gpsimd.memset(spread1[2][:], 0.0)
-        zeros = warm[:, 0:1].to_broadcast([P, T])
-        spread2 = [held("spread2_0", [P, T], F32)]
-        nc.scalar.copy(spread2[0][:], zeros)
+        make_identity(nc, ident[:])
+        spread2 = [held(f"spread2_{i}", [P, T], F32) for i in range(2)]
+        nc.gpsimd.memset(spread2[0][:], 0.0)
+        nc.scalar.copy(spread2[1][:], warm[:, 0:1].to_broadcast([P, T]))
         for t in (A, B, C, L):
             nc.sync.dma_start(res[t][:], xr_v[:, t, :])
+        nc.sync.dma_start(idx2[:], offs2)
+        load_scale_rows(w2s_raw, w2_scales)
+        nc.sync.dma_start(w2_raw[:], w2_words[0].rearrange("p n d -> p (n d)").bitcast(I32))
         nc.sync.dma_start(g2[:], gate2)
 
         nc.vector.tensor_copy(gs[:], xs[:].indirect(idx1[:]))
-        nc.vector.tensor_copy(gw[:], xw[:].bitcast(U32).indirect(idx1[:]))
-        src = [w1_raw[h][:].rearrange("p j (m t) -> p m t j", t=PACK) for h in range(2)]
-        dst = w1_bf[:].rearrange("p (u m j) -> p m u j", u=2, j=PACK)
-        nc.scalar.copy(dst[:, 0:64], src[0][:, :, 1:3])
-        nc.scalar.copy(dst[:, 64:128, 1], src[1][:, :, 2])
-        nc.vector.tensor_copy(dst[:, 64:128, 0], src[1][:, :, 1])
-        slot1 = {A: 0, B: 1, C: 2, L: 3}
-        for t, u in ((A, 1), (B, 0)):
-            w_cols = slice(slot1[t] * P, (slot1[t] + 1) * P)
-            nc.vector.quantize_mx(out=w1_q[:, w_cols].bitcast(FP8X4), scales=w1_s[:, w_cols], in_=w1_bf[:, u * K : (u + 1) * K])
-        w1_bf2 = held("w1_bf2", [P, 2 * K], BF16, "w1_bf")
-        dst2 = w1_bf2[:].rearrange("p (u m j) -> p m u j", u=2, j=PACK)
+        dst = w1_bf[:].rearrange("p (t m j) -> p m t j", t=PACK, j=PACK)
         for h in range(2):
-            nc.vector.tensor_copy(dst2[:, 64 * h : 64 * (h + 1)], src[h][:, :, 0:4:3])
-        nc.vector.quantize_mx(out=w1_q[:, 2 * P :].bitcast(FP8X4), scales=w1_s[:, 2 * P :], in_=w1_bf2[:])
-        w2_q = held("w2_q", [P, K], I32, "w1_bf")
-        w2_s = held("w2_s", [P, K], U8, "w1_raw1")
-        nc.vector.tensor_copy(w2_s[:].rearrange("p (t m) -> p t m", t=PACK), w2s_raw[:].rearrange("p (m t) -> p t m", t=PACK))
-        nc.vector.tensor_copy(w2_q[:].rearrange("p (t m) -> p t m", t=PACK), w2_raw[:].rearrange("p (m t) -> p t m", t=PACK))
+            nc.scalar.copy(dst[:, 64 * h : 64 * (h + 1)], w1_raw[h][:].rearrange("p j (m t) -> p m t j", t=PACK))
+        nc.vector.quantize_mx(out=w1_q[:].bitcast(FP8X4), scales=w1_s[:], in_=w1_bf[:])
+        for c, m in ((0, 1), (1, 3)):
+            nc.vector.tensor_copy(gw[:, cols(c, m)], xw[:].bitcast(U32).indirect(entries(idx1, c, m)))
 
-        def product(wq, ws, slot, codes, scales, dst, c, n):
-            acc = mm_ps.tile([P, n * CH], F32, name="acc")
+        def bank(half, g):
+            return psum.tile([P, BANK], F32, name=f"bank{half}_{g}")
+
+        def product(acc, wq, ws, slot, codes, scales, dst, c, n):
             w_cols = slice(slot * P, (slot + 1) * P)
             nc.tensor.matmul_mx(
-                out=acc[:],
+                out=acc[:, : n * CH],
                 lhsT=wq[:, w_cols].bitcast(FP8X4),
                 lhsT_scale=ws[:, w_cols],
                 rhs=codes[:, cols(c, n)].bitcast(FP8X4),
@@ -133,64 +131,93 @@ def tile_moe_mod_silu_kernel(
                 start=True,
                 stop=True,
             )
-            nc.scalar.activation(dst[:, cols(c, n)], acc[:], SILU)
+            nc.scalar.activation(dst[:, cols(c, n)], acc[:, : n * CH], SILU)
 
-        def gated(values, gate, c, n):
-            nc.gpsimd.tensor_tensor(values[:, cols(c, n)], values[:, cols(c, n)], gate[:, cols(c, n)], MULT)
+        def scatter(window, idx, values, gate, c, n):
+            nc.vector.tensor_tensor(window[:].indirect(entries(idx, c, n)), values[:, cols(c, n)], gate[:, cols(c, n)], MULT)
 
-        def scatter(window, idx, values, c, n):
-            nc.vector.tensor_copy(window[:].indirect(entries(idx, c, n)), values[:, cols(c, n)])
+        def turn(acc, src, start, stop):
+            for b in range(BLOCKS):
+                blk = slice(b * P, (b + 1) * P)
+                nc.tensor.matmul(
+                    acc[:, blk], src[:, blk], ident[:], start=start and b == 0, stop=stop and b == BLOCKS - 1, is_transpose=True
+                )
 
-        def layer(wq, ws, slot, codes, scales, values, gate, idx, spread):
-            for t, pieces in ((A, ((0, 1),)), (B, ((0, 1),)), (A, ((1, 1), (2, 2))), (B, ((1, 1), (2, 2))), (C, ((0, 2), (2, 2))), (L, ((0, 2), (2, 2)))):
-                for c, n in pieces:
-                    product(wq, ws, slot[t], codes, scales, values[t], c, n)
-                first, count = pieces[0][0], sum(n for c, n in pieces)
-                gated(values[t], gate, first, count)
-                if t != L:
-                    scatter(spread[slot1[t]], idx, values[t], first, count)
+        def span(g):
+            return slice(g * BANK, (g + 1) * BANK)
 
-        layer(w1_q, w1_s, slot1, gw, gs, y, g1, idx1, spread1)
-        spread2.append(held("spread2_1", [P, T], F32, "gw"))
-        spread2.append(held("spread2_2", [P, T], F32, "w1_q"))
-        nc.scalar.copy(spread2[1][:], zeros)
-        nc.scalar.copy(spread2[2][:], zeros)
+        order = (A, B, C, L)
+        passes = ((A, 0, 1), (A, 1, 1), (A, 2, 2)) + tuple((t, c, 2) for t in order[1:] for c in (0, 2))
+        for i, (t, c, m) in enumerate(passes):
+            product(bank(1, i % SPANS), w1_q, w1_s, t, gw, gs, y[t], c, m)
 
-        r = {}
+        r_turned = {}
         r16 = {}
-        for t, width in ((A, 1024), (B, 1024), (C, 512)):
-            r[t] = held(f"r{t}", [P, T], F32, f"r16_{A}" if t == C else None)
+        for n, t in enumerate(order[:3]):
+            window = spread1[n % 2]
+            sums = [bank(n % 2, g) for g in range(SPANS)]
+            for g in range(SPANS):
+                turn(sums[g], res[t][:, span(g)], True, False)
+            for c, m in ((0, 1), (1, 3)) if t == A else ((0, NCH),):
+                scatter(window, idx1, y[t], g1, c, m)
+            r_turned[t] = held(f"r_turned{t}", [P, T], F32, f"r16_{order[n - 1]}" if n else None)
             r16[t] = held(f"r16_{t}", [P, T], BF16)
-            for lo in range(0, T, width):
-                span = slice(lo, lo + width)
-                nc.gpsimd.tensor_tensor(r[t][:, span], res[t][:, span], spread1[slot1[t]][:, span], ADD)
-                nc.scalar.copy(r16[t][:, span], r[t][:, span])
-            if t == A:
-                scatter(spread1[0], idx1, y[L], 0, NCH)
-            for c, n in (((0, NCH),) if t != C else tuple((c, 1) for c in range(NCH))):
-                nc.scalar.activation(rb_v[:, cols(c, n), t], r16[t][:].indirect(entries(idx2, c, n)), COPY)
-        r[L] = held("r_last", [P, T], F32, "spread1_2")
-        nc.vector.tensor_tensor(r[L][:], res[L][:], spread1[0][:], ADD)
+            for g in range(SPANS):
+                turn(sums[g], window[:, span(g)], False, True)
+                nc.scalar.copy(r_turned[t][:, span(g)], sums[g][:])
+            for g in range(SPANS):
+                back = bank(1 - n % 2, g)
+                turn(back, r_turned[t][:, span(g)], True, True)
+                nc.scalar.copy(r16[t][:, span(g)], back[:])
+            for c in range(NCH):
+                nc.scalar.activation(in_pair(c, t), r16[t][:].indirect(entries(idx2, c)), COPY)
+        scatter(spread1[1], idx1, y[L], g1, 0, NCH)
+        r_last = held("r_last", [P, T], F32, "spread1_0")
+        nc.vector.tensor_tensor(r_last[:], res[L][:], spread1[1][:], ADD)
 
+        w2_q = held("w2_q", [P, K], I32, f"res{L}")
+        w2_s = held("w2_s", [P, K], U8, "spread1_1")
+        nc.vector.tensor_copy(w2_q[:].rearrange("p (t m) -> p t m", t=PACK), w2_raw[:].rearrange("p (m t) -> p t m", t=PACK))
         for c in range(NCH):
-            nc.vector.tensor_copy(rb_v[:, cols(c), L], r[L][:].indirect(entries(idx2, c)))
+            nc.vector.tensor_copy(in_pair(c, L), r_last[:].indirect(entries(idx2, c)))
+            if c == 1:
+                nc.vector.tensor_copy(w2_s[:].rearrange("p (t m) -> p t m", t=PACK), w2s_raw[:].rearrange("p (m t) -> p t m", t=PACK))
+            if c:
+                nc.scalar.copy(
+                    rb[c][:].bitcast(U32).rearrange("p (s u) -> p s u", u=2),
+                    pairs[c - 1][:].bitcast(U32).rearrange("p (u s) -> p s u", u=2),
+                )
             nc.vector.quantize_mx(
                 out=rq[:, cols(c)].bitcast(FP8X4),
                 scales=rs[:, cols(c)],
-                in_=rb[:, c * CH * PACK : (c + 1) * CH * PACK],
+                in_=rb[c][:],
             )
-        layer(w2_q, w2_s, {t: t for t in range(PACK)}, rq, rs, z, g2, idx2, spread2)
-        for t, width, tag in ((A, 1024, f"res{A}"), (B, 1024, f"res{L}"), (C, 512, "xw")):
-            done = held(f"done{t}", [P, T], F32, tag)
-            for lo in range(0, T, width):
-                span = slice(lo, lo + width)
-                nc.gpsimd.tensor_tensor(done[:, span], r[t][:, span], spread2[slot1[t]][:, span], ADD)
-                nc.sync.dma_start(out_v[:, t, span], done[:, span])
-            if t == A:
-                scatter(spread2[0], idx2, z[L], 0, NCH)
-        done_last = held("done_last", [P, T], F32, "w1_q")
+        passes = ((A, 0, 1), (B, 0, 1), (A, 1, 1), (A, 2, 2), (B, 1, 1), (B, 2, 2), (C, 0, 2), (C, 2, 2), (L, 0, 2), (L, 2, 2))
+        for i, (t, c, m) in enumerate(passes):
+            product(bank(0, i % SPANS), w2_q, w2_s, t, rq, rs, z[t], c, m)
+        for t, c, m in ((A, 0, 1), (B, 0, 1), (A, 1, 3), (B, 1, 3)):
+            scatter(spread2[order.index(t)], idx2, z[t], g2, c, m)
+        for n, t in enumerate(order[:3]):
+            window = spread2[n % 2]
+            if t == C:
+                scatter(window, idx2, z[t], g2, 0, NCH)
+            sums = [bank(1 - n % 2, g) for g in range(SPANS)]
+            for g in range(SPANS):
+                turn(sums[g], r_turned[t][:, span(g)], True, False)
+            turned = [held(f"turned{t}_{g}", [P, BANK], F32, f"turned{g}") for g in range(SPANS)]
+            for g in range(SPANS):
+                there = bank(n % 2, g)
+                turn(there, window[:, span(g)], True, True)
+                nc.scalar.copy(turned[g][:], there[:])
+            for g in range(SPANS):
+                turn(sums[g], turned[g][:], False, True)
+                done = held(f"done{t}_{g}", [P, BANK], F32, f"done{g}")
+                nc.scalar.copy(done[:], sums[g][:])
+                nc.sync.dma_start(out_v[:, t, span(g)], done[:])
+        scatter(spread2[1], idx2, z[L], g2, 0, NCH)
+        done_last = held("done_last", [P, T], F32, "turned3")
         edges = (0, 256, 768, 1280, 1792, 2048)
         for lo, hi in zip(edges, edges[1:]):
-            span = slice(lo, hi)
-            nc.vector.tensor_tensor(done_last[:, span], r[L][:, span], spread2[0][:, span], ADD)
-            nc.sync.dma_start(out_v[:, L, span], done_last[:, span])
+            part = slice(lo, hi)
+            nc.vector.tensor_tensor(done_last[:, part], r_last[:, part], spread2[1][:, part], ADD)
+            nc.scalar.dma_start(out_v[:, L, part], done_last[:, part])

@@ -84,9 +84,7 @@ def tile_moe_mod_silu_kernel(
             for q in range(4):
                 nc.sync.dma_start(plane[32 * q : 32 * q + 4, :].bitcast(I32), rows[0, 4 * q : 4 * q + 4, :].bitcast(I32))
 
-        nc.gpsimd.memset(xs[:, : T // 2].bitcast(I32), 0)
-        nc.vector.memset(xs[:, T // 2 :].bitcast(I32), 0)
-        nc.gpsimd.memset(w2s_raw[:].bitcast(I32), 0)
+        nc.gpsimd.memset(xs[:].bitcast(I32), 0)
         nc.sync.dma_start(w1_raw[0][:], w1_v[:, :, cols(0)])
         nc.sync.dma_start(idx1[:], offs)
         load_scale_rows(xs, x_scales)
@@ -96,12 +94,13 @@ def tile_moe_mod_silu_kernel(
         nc.sync.dma_start(xw[:], x_words[0].rearrange("p c d -> p (c d)").bitcast(I32))
         nc.sync.dma_start(g1[:, cols(0)], gate1[:, cols(0)])
         nc.sync.dma_start(g1[:, cols(1, 3)], gate1[:, cols(1, 3)])
-        nc.gpsimd.memset(spread1[0][:], 0.0)
-        nc.gpsimd.memset(spread1[1][:], 0.0)
         make_identity(nc, ident[:])
-        spread2 = [held(f"spread2_{i}", [P, T], F32) for i in range(2)]
-        nc.gpsimd.memset(spread2[0][:], 0.0)
-        nc.scalar.copy(spread2[1][:], warm[:, 0:1].to_broadcast([P, T]))
+        nc.vector.memset(w2s_raw[:].bitcast(I32), 0)
+        nc.vector.memset(spread1[0][:], 0.0)
+        nc.vector.memset(spread1[1][:], 0.0)
+        zeros = warm[:, 0:1].to_broadcast([P, T])
+        spread2 = [held("spread2_0", [P, T], F32)]
+        nc.scalar.copy(spread2[0][:], zeros)
         for t in (A, B, C, L):
             nc.sync.dma_start(res[t][:], xr_v[:, t, :])
         nc.sync.dma_start(idx2[:], offs2)
@@ -150,6 +149,9 @@ def tile_moe_mod_silu_kernel(
         passes = ((A, 0, 1), (A, 1, 1), (A, 2, 2)) + tuple((t, c, 2) for t in order[1:] for c in (0, 2))
         for i, (t, c, m) in enumerate(passes):
             product(bank(1, i % SPANS), w1_q, w1_s, t, gw, gs, y[t], c, m)
+
+        spread2.append(held("spread2_1", [P, T], F32, "gw"))
+        nc.scalar.copy(spread2[1][:], zeros)
 
         r_turned = {}
         r16 = {}

@@ -26,6 +26,8 @@ BANK = 512
 BLOCKS = BANK // P
 SPANS = T // BANK
 A, B, C, L = 2, 1, 0, 3
+ORDER = (A, B, C, L)
+LAST_EDGES = (0, 128, 640, 1152, 1664, 1920, 2048)
 FLOPS = 2 * 2 * K * K * S
 
 
@@ -52,15 +54,15 @@ def tile_moe_mod_silu_kernel(
         w2s_raw = held("w2s_raw", [P, K], U8)
         g1 = held("g1", [P, S], F32)
         g2 = held("g2", [P, S], F32)
-        warm = held("warm", [P, 8], F32)
+        zero = held("zero", [P, 2], F32)
         res = [held(f"res{t}", [P, T], F32) for t in range(PACK)]
-        spread1 = [held(f"spread1_{i}", [P, T], F32) for i in range(2)]
+        spread1 = [held("spread1_0", [P, T], F32)]
         ident = held("ident", [P, P], F32)
         gw = held("gw", [P, S], U32)
         gs = held("gs", [P, S], U8)
         y = [held(f"y{t}", [P, S], F32) for t in range(PACK)]
         z = [held(f"z{t}", [P, S], F32) for t in range(PACK)]
-        pairs = [held(f"pairs{c}", [P, CH * PACK], BF16) for c in range(1, NCH)]
+        pairs = [held(f"pairs{c}", [P, CH * PACK], BF16) for c in range(NCH)]
         rb = [held(f"rb{c}", [P, CH * PACK], BF16) for c in range(NCH)]
         rq = held("rq", [P, S], U32)
         rs = held("rs", [P, S], U8)
@@ -76,32 +78,28 @@ def tile_moe_mod_silu_kernel(
             return idx[:, c * CH // 16 : (c + n) * CH // 16]
 
         def in_pair(c, t):
-            if c == 0:
-                return rb[0][:].rearrange("p (s t) -> p s t", t=PACK)[:, :, t]
-            return pairs[c - 1][:].rearrange("p (u s e) -> p u s e", u=2, e=2)[:, t // 2, :, t % 2]
+            return pairs[c][:].rearrange("p (u s e) -> p u s e", u=2, e=2)[:, t // 2, :, t % 2]
 
-        def load_scale_rows(plane, rows):
+        def load_scale_rows(scale_tile, rows):
             for q in range(4):
-                nc.sync.dma_start(plane[32 * q : 32 * q + 4, :].bitcast(I32), rows[0, 4 * q : 4 * q + 4, :].bitcast(I32))
+                nc.sync.dma_start(
+                    scale_tile[32 * q : 32 * q + 4, :].bitcast(I32), rows[0, 4 * q : 4 * q + 4, :].bitcast(I32)
+                )
 
         nc.gpsimd.memset(xs[:].bitcast(I32), 0)
-        nc.sync.dma_start(w1_raw[0][:], w1_v[:, :, cols(0)])
+        nc.sync.dma_start(w1_raw[0][:], w1_v[:, :, : K // 2])
         nc.sync.dma_start(idx1[:], offs)
         load_scale_rows(xs, x_scales)
-        nc.vector.memset(warm[:], 0.0)
-        nc.scalar.activation(warm[:, 4:8], warm[:, 0:4], SILU)
-        nc.sync.dma_start(w1_raw[1][:], w1_v[:, :, cols(1)])
+        nc.vector.memset(zero[:, 0:1], 0.0)
+        nc.scalar.activation(zero[:, 1:2], zero[:, 0:1], SILU)
+        nc.sync.dma_start(w1_raw[1][:], w1_v[:, :, K // 2 :])
         nc.sync.dma_start(xw[:], x_words[0].rearrange("p c d -> p (c d)").bitcast(I32))
         nc.sync.dma_start(g1[:, cols(0)], gate1[:, cols(0)])
-        nc.sync.dma_start(g1[:, cols(1, 3)], gate1[:, cols(1, 3)])
+        nc.sync.dma_start(g1[:, cols(1, NCH - 1)], gate1[:, cols(1, NCH - 1)])
         make_identity(nc, ident[:])
         nc.vector.memset(w2s_raw[:].bitcast(I32), 0)
         nc.vector.memset(spread1[0][:], 0.0)
-        nc.vector.memset(spread1[1][:], 0.0)
-        zeros = warm[:, 0:1].to_broadcast([P, T])
-        spread2 = [held("spread2_0", [P, T], F32)]
-        nc.scalar.copy(spread2[0][:], zeros)
-        for t in (A, B, C, L):
+        for t in ORDER:
             nc.sync.dma_start(res[t][:], xr_v[:, t, :])
         nc.sync.dma_start(idx2[:], offs2)
         load_scale_rows(w2s_raw, w2_scales)
@@ -109,18 +107,24 @@ def tile_moe_mod_silu_kernel(
         nc.sync.dma_start(g2[:], gate2)
 
         nc.vector.tensor_copy(gs[:], xs[:].indirect(idx1[:]))
-        dst = w1_bf[:].rearrange("p (t m j) -> p m t j", t=PACK, j=PACK)
+        w1_dst = w1_bf[:].rearrange("p (t m j) -> p m t j", t=PACK, j=PACK)
         for h in range(2):
-            nc.scalar.copy(dst[:, 64 * h : 64 * (h + 1)], w1_raw[h][:].rearrange("p j (m t) -> p m t j", t=PACK))
+            nc.scalar.copy(
+                w1_dst[:, P // 2 * h : P // 2 * (h + 1)], w1_raw[h][:].rearrange("p j (m t) -> p m t j", t=PACK)
+            )
+        zeros = zero[:, 1:2].to_broadcast([P, T])
+        spread1.append(held("spread1_1", [P, T], F32, "w1_raw1"))
+        nc.scalar.copy(spread1[1][:], zeros)
         nc.vector.quantize_mx(out=w1_q[:].bitcast(FP8X4), scales=w1_s[:], in_=w1_bf[:])
-        for c, m in ((0, 1), (1, 3)):
-            nc.vector.tensor_copy(gw[:, cols(c, m)], xw[:].bitcast(U32).indirect(entries(idx1, c, m)))
+        first_and_rest = ((0, 1), (1, NCH - 1))
+        for c, n in first_and_rest:
+            nc.vector.tensor_copy(gw[:, cols(c, n)], xw[:].bitcast(U32).indirect(entries(idx1, c, n)))
 
         def bank(half, g):
             return psum.tile([P, BANK], F32, name=f"bank{half}_{g}")
 
-        def product(acc, wq, ws, slot, codes, scales, dst, c, n):
-            w_cols = slice(slot * P, (slot + 1) * P)
+        def product(acc, wq, ws, t, codes, scales, dst, c, n):
+            w_cols = slice(t * P, (t + 1) * P)
             nc.tensor.matmul_mx(
                 out=acc[:, : n * CH],
                 lhsT=wq[:, w_cols].bitcast(FP8X4),
@@ -133,42 +137,49 @@ def tile_moe_mod_silu_kernel(
             nc.scalar.activation(dst[:, cols(c, n)], acc[:, : n * CH], SILU)
 
         def scatter(window, idx, values, gate, c, n):
-            nc.vector.tensor_tensor(window[:].indirect(entries(idx, c, n)), values[:, cols(c, n)], gate[:, cols(c, n)], MULT)
+            nc.vector.tensor_tensor(
+                window[:].indirect(entries(idx, c, n)), values[:, cols(c, n)], gate[:, cols(c, n)], MULT
+            )
 
         def turn(acc, src, start, stop):
             for b in range(BLOCKS):
                 blk = slice(b * P, (b + 1) * P)
                 nc.tensor.matmul(
-                    acc[:, blk], src[:, blk], ident[:], start=start and b == 0, stop=stop and b == BLOCKS - 1, is_transpose=True
+                    acc[:, blk],
+                    src[:, blk],
+                    ident[:],
+                    start=start and b == 0,
+                    stop=stop and b == BLOCKS - 1,
+                    is_transpose=True,
                 )
 
         def span(g):
             return slice(g * BANK, (g + 1) * BANK)
 
-        order = (A, B, C, L)
-        passes = ((A, 0, 1), (A, 1, 1), (A, 2, 2)) + tuple((t, c, 2) for t in order[1:] for c in (0, 2))
-        for i, (t, c, m) in enumerate(passes):
-            product(bank(1, i % SPANS), w1_q, w1_s, t, gw, gs, y[t], c, m)
+        passes1 = ((A, 0, 1), (A, 1, 1), (A, 2, 2)) + tuple((t, c, 2) for t in ORDER[1:] for c in (0, 2))
+        for i, (t, c, n) in enumerate(passes1):
+            product(bank(1, i % SPANS), w1_q, w1_s, t, gw, gs, y[t], c, n)
 
-        spread2.append(held("spread2_1", [P, T], F32, "gw"))
-        nc.scalar.copy(spread2[1][:], zeros)
+        spread2 = [held("spread2_0", [P, T], F32, "gw"), held("spread2_1", [P, T], F32)]
+        nc.scalar.copy(spread2[0][:], zeros)
+        nc.sync.dma_start(spread2[1][:], spread2[0][:])
 
         r_turned = {}
         r16 = {}
-        for n, t in enumerate(order[:3]):
-            window = spread1[n % 2]
-            sums = [bank(n % 2, g) for g in range(SPANS)]
+        for i, t in enumerate(ORDER[:-1]):
+            window = spread1[i % 2]
+            sums = [bank(i % 2, g) for g in range(SPANS)]
             for g in range(SPANS):
                 turn(sums[g], res[t][:, span(g)], True, False)
-            for c, m in ((0, 1), (1, 3)) if t == A else ((0, NCH),):
-                scatter(window, idx1, y[t], g1, c, m)
-            r_turned[t] = held(f"r_turned{t}", [P, T], F32, f"r16_{order[n - 1]}" if n else None)
+            for c, n in first_and_rest if t == A else ((0, NCH),):
+                scatter(window, idx1, y[t], g1, c, n)
+            r_turned[t] = held(f"r_turned{t}", [P, T], F32, f"r16_{A}" if t == B else None)
             r16[t] = held(f"r16_{t}", [P, T], BF16)
             for g in range(SPANS):
                 turn(sums[g], window[:, span(g)], False, True)
                 nc.scalar.copy(r_turned[t][:, span(g)], sums[g][:])
             for g in range(SPANS):
-                back = bank(1 - n % 2, g)
+                back = bank(1 - i % 2, g)
                 turn(back, r_turned[t][:, span(g)], True, True)
                 nc.scalar.copy(r16[t][:, span(g)], back[:])
             for c in range(NCH):
@@ -178,37 +189,49 @@ def tile_moe_mod_silu_kernel(
         nc.vector.tensor_tensor(r_last[:], res[L][:], spread1[1][:], ADD)
 
         w2_q = held("w2_q", [P, K], I32, f"res{L}")
-        w2_s = held("w2_s", [P, K], U8, "spread1_1")
-        nc.vector.tensor_copy(w2_q[:].rearrange("p (t m) -> p t m", t=PACK), w2_raw[:].rearrange("p (m t) -> p t m", t=PACK))
-        for c in range(NCH):
-            nc.vector.tensor_copy(in_pair(c, L), r_last[:].indirect(entries(idx2, c)))
-            if c == 1:
-                nc.vector.tensor_copy(w2_s[:].rearrange("p (t m) -> p t m", t=PACK), w2s_raw[:].rearrange("p (m t) -> p t m", t=PACK))
-            if c:
-                nc.scalar.copy(
-                    rb[c][:].bitcast(U32).rearrange("p (s u) -> p s u", u=2),
-                    pairs[c - 1][:].bitcast(U32).rearrange("p (u s) -> p s u", u=2),
-                )
-            nc.vector.quantize_mx(
-                out=rq[:, cols(c)].bitcast(FP8X4),
-                scales=rs[:, cols(c)],
-                in_=rb[c][:],
+        w2_s = held("w2_s", [P, K], U8, "w1_raw1")
+
+        def to_planes(dst, src):
+            nc.vector.tensor_copy(
+                dst[:].rearrange("p (t m) -> p m t", t=PACK), src[:].rearrange("p (m t) -> p m t", t=PACK)
             )
-        passes = ((A, 0, 1), (B, 0, 1), (A, 1, 1), (A, 2, 2), (B, 1, 1), (B, 2, 2), (C, 0, 2), (C, 2, 2), (L, 0, 2), (L, 2, 2))
-        for i, (t, c, m) in enumerate(passes):
-            product(bank(0, i % SPANS), w2_q, w2_s, t, rq, rs, z[t], c, m)
-        for t, c, m in ((A, 0, 1), (B, 0, 1), (A, 1, 3), (B, 1, 3)):
-            scatter(spread2[order.index(t)], idx2, z[t], g2, c, m)
-        for n, t in enumerate(order[:3]):
-            window = spread2[n % 2]
+
+        def gather_last(c):
+            nc.vector.tensor_copy(in_pair(c, L), r_last[:].indirect(entries(idx2, c)))
+
+        def quantise(c):
+            nc.scalar.copy(
+                rb[c][:].bitcast(U32).rearrange("p (s u) -> p s u", u=2),
+                pairs[c][:].bitcast(U32).rearrange("p (u s) -> p s u", u=2),
+            )
+            nc.vector.quantize_mx(out=rq[:, cols(c)].bitcast(FP8X4), scales=rs[:, cols(c)], in_=rb[c][:])
+
+        to_planes(w2_q, w2_raw)
+        gather_last(0)
+        quantise(0)
+        gather_last(1)
+        to_planes(w2_s, w2s_raw)
+        quantise(1)
+        for c in range(2, NCH):
+            gather_last(c)
+            quantise(c)
+        passes2 = ((A, 0, 1), (B, 0, 1)) + tuple((t, c, n) for t in (A, B) for c, n in ((1, 1), (2, 2)))
+        passes2 = passes2 + tuple((t, c, 2) for t in (C, L) for c in (0, 2))
+        for i, (t, c, n) in enumerate(passes2):
+            product(bank(0, i % SPANS), w2_q, w2_s, t, rq, rs, z[t], c, n)
+        for c, n in first_and_rest:
+            for i, t in enumerate((A, B)):
+                scatter(spread2[i], idx2, z[t], g2, c, n)
+        for i, t in enumerate(ORDER[:-1]):
+            window = spread2[i % 2]
             if t == C:
                 scatter(window, idx2, z[t], g2, 0, NCH)
-            sums = [bank(1 - n % 2, g) for g in range(SPANS)]
+            sums = [bank(1 - i % 2, g) for g in range(SPANS)]
             for g in range(SPANS):
                 turn(sums[g], r_turned[t][:, span(g)], True, False)
             turned = [held(f"turned{t}_{g}", [P, BANK], F32, f"turned{g}") for g in range(SPANS)]
             for g in range(SPANS):
-                there = bank(n % 2, g)
+                there = bank(i % 2, g)
                 turn(there, window[:, span(g)], True, True)
                 nc.scalar.copy(turned[g][:], there[:])
             for g in range(SPANS):
@@ -217,9 +240,8 @@ def tile_moe_mod_silu_kernel(
                 nc.scalar.copy(done[:], sums[g][:])
                 nc.sync.dma_start(out_v[:, t, span(g)], done[:])
         scatter(spread2[1], idx2, z[L], g2, 0, NCH)
-        done_last = held("done_last", [P, T], F32, "turned3")
-        edges = (0, 256, 768, 1280, 1792, 2048)
-        for lo, hi in zip(edges, edges[1:]):
+        done_last = held("done_last", [P, T], F32, f"turned{SPANS - 1}")
+        for lo, hi in zip(LAST_EDGES, LAST_EDGES[1:]):
             part = slice(lo, hi)
             nc.vector.tensor_tensor(done_last[:, part], r_last[:, part], spread2[1][:, part], ADD)
             nc.scalar.dma_start(out_v[:, L, part], done_last[:, part])

@@ -95,15 +95,21 @@ def tile_moe_mod_silu_kernel(
         nc.sync.dma_start(w1_raw[1][:], w1_v[:, :, K // 2 :])
         nc.sync.dma_start(xw[:], x_words[0].rearrange("p c d -> p (c d)").bitcast(I32))
         nc.sync.dma_start(g1[:, cols(0)], gate1[:, cols(0)])
+        nc.vector.memset(w2s_raw[:].bitcast(I32), 0)
+        nc.sync.dma_start(w2_raw[:], w2_words[0].rearrange("p n d -> p (n d)").bitcast(I32))
+        load_scale_rows(w2s_raw, w2_scales)
         nc.sync.dma_start(g1[:, cols(1, NCH - 1)], gate1[:, cols(1, NCH - 1)])
         make_identity(nc, ident[:])
-        nc.vector.memset(w2s_raw[:].bitcast(I32), 0)
+        w2_q = held("w2_q", [P, K], I32)
+        w2_s = held("w2_s", [P, K], U8)
+        for dst, src in ((w2_q, w2_raw), (w2_s, w2s_raw)):
+            nc.gpsimd.tensor_copy(
+                dst[:].rearrange("p (t m) -> p t m", t=PACK), src[:].rearrange("p (m t) -> p t m", t=PACK)
+            )
         nc.vector.memset(spread1[0][:], 0.0)
         for t in ORDER:
             nc.sync.dma_start(res[t][:], xr_v[:, t, :])
         nc.sync.dma_start(idx2[:], offs2)
-        load_scale_rows(w2s_raw, w2_scales)
-        nc.sync.dma_start(w2_raw[:], w2_words[0].rearrange("p n d -> p (n d)").bitcast(I32))
         nc.sync.dma_start(g2[:], gate2)
 
         nc.vector.tensor_copy(gs[:], xs[:].indirect(idx1[:]))
@@ -188,14 +194,6 @@ def tile_moe_mod_silu_kernel(
         r_last = held("r_last", [P, T], F32, "spread1_0")
         nc.vector.tensor_tensor(r_last[:], res[L][:], spread1[1][:], ADD)
 
-        w2_q = held("w2_q", [P, K], I32, f"res{L}")
-        w2_s = held("w2_s", [P, K], U8, "w1_raw1")
-
-        def to_planes(dst, src):
-            nc.vector.tensor_copy(
-                dst[:].rearrange("p (t m) -> p m t", t=PACK), src[:].rearrange("p (m t) -> p m t", t=PACK)
-            )
-
         def gather_last(c):
             nc.vector.tensor_copy(in_pair(c, L), r_last[:].indirect(entries(idx2, c)))
 
@@ -206,11 +204,9 @@ def tile_moe_mod_silu_kernel(
             )
             nc.vector.quantize_mx(out=rq[:, cols(c)].bitcast(FP8X4), scales=rs[:, cols(c)], in_=rb[c][:])
 
-        to_planes(w2_q, w2_raw)
         gather_last(0)
         quantise(0)
         gather_last(1)
-        to_planes(w2_s, w2s_raw)
         quantise(1)
         for c in range(2, NCH):
             gather_last(c)

@@ -27,7 +27,7 @@ BLOCKS = BANK // P
 SPANS = T // BANK
 A, B, C, L = 2, 1, 0, 3
 ORDER = (A, B, C, L)
-LAST_EDGES = (0, 128, 640, 1152, 1664, 1920, 2048)
+LAST_EDGES = (0, 128, 384, 768, 1280, 1792, 2048)
 FLOPS = 2 * 2 * K * K * S
 
 

@@ -62,7 +62,9 @@ def tile_moe_mod_silu_kernel(
         gs = held("gs", [P, S], U8)
         y = [held(f"y{t}", [P, S], F32) for t in range(PACK)]
         z = [held(f"z{t}", [P, S], F32) for t in range(PACK)]
-        pairs = [held(f"pairs{c}", [P, CH * PACK], BF16) for c in range(NCH)]
+        shared = held("shared", [P, CH * (2 * PACK - 1)], BF16)
+        rows_last = shared[:, : CH * PACK]
+        pairs = [shared[:, CH * (PACK - 1) :]] + [held(f"pairs{c}", [P, CH * PACK], BF16)[:] for c in range(1, NCH - 1)]
         rb = [held(f"rb{c}", [P, CH * PACK], BF16) for c in range(NCH)]
         rq = held("rq", [P, S], U32)
         rs = held("rs", [P, S], U8)
@@ -78,7 +80,9 @@ def tile_moe_mod_silu_kernel(
             return idx[:, c * CH // 16 : (c + n) * CH // 16]
 
         def in_pair(c, t):
-            return pairs[c][:].rearrange("p (u s e) -> p u s e", u=2, e=2)[:, t // 2, :, t % 2]
+            if c == NCH - 1:
+                return rows_last[:, cols(t)]
+            return pairs[c].rearrange("p (u s e) -> p u s e", u=2, e=2)[:, t // 2, :, t % 2]
 
         def load_scale_rows(scale_tile, rows):
             for q in range(4):
@@ -123,7 +127,8 @@ def tile_moe_mod_silu_kernel(
         nc.scalar.copy(spread1[1][:], zeros)
         nc.vector.quantize_mx(out=w1_q[:].bitcast(FP8X4), scales=w1_s[:], in_=w1_bf[:])
         first_and_rest = ((0, 1), (1, NCH - 1))
-        for c, n in first_and_rest:
+        first_middle_last = ((0, 1), (1, NCH - 2), (NCH - 1, 1))
+        for c, n in first_middle_last:
             nc.vector.tensor_copy(gw[:, cols(c, n)], xw[:].bitcast(U32).indirect(entries(idx1, c, n)))
 
         def bank(half, g):
@@ -162,7 +167,7 @@ def tile_moe_mod_silu_kernel(
         def span(g):
             return slice(g * BANK, (g + 1) * BANK)
 
-        passes1 = ((A, 0, 1), (A, 1, 1), (A, 2, 2)) + tuple((t, c, 2) for t in ORDER[1:] for c in (0, 2))
+        passes1 = tuple((A, c, n) for c, n in first_middle_last) + tuple((t, c, 2) for t in ORDER[1:] for c in (0, 2))
         for i, (t, c, n) in enumerate(passes1):
             product(bank(1, i % SPANS), w1_q, w1_s, t, gw, gs, y[t], c, n)
 
@@ -198,23 +203,27 @@ def tile_moe_mod_silu_kernel(
             nc.vector.tensor_copy(in_pair(c, L), r_last[:].indirect(entries(idx2, c)))
 
         def quantise(c):
-            nc.scalar.copy(
-                rb[c][:].bitcast(U32).rearrange("p (s u) -> p s u", u=2),
-                pairs[c][:].bitcast(U32).rearrange("p (u s) -> p s u", u=2),
-            )
+            if c == NCH - 1:
+                nc.scalar.copy(
+                    rb[c][:].rearrange("p (s t) -> p s t", t=PACK), rows_last.rearrange("p (t s) -> p s t", t=PACK)
+                )
+            else:
+                nc.scalar.copy(
+                    rb[c][:].bitcast(U32).rearrange("p (s u) -> p s u", u=2),
+                    pairs[c].bitcast(U32).rearrange("p (u s) -> p s u", u=2),
+                )
             nc.vector.quantize_mx(out=rq[:, cols(c)].bitcast(FP8X4), scales=rs[:, cols(c)], in_=rb[c][:])
 
-        gather_last(0)
-        quantise(0)
-        gather_last(1)
-        quantise(1)
-        for c in range(2, NCH):
+        for c in range(NCH - 1):
             gather_last(c)
             quantise(c)
-        passes2 = ((A, 0, 1), (B, 0, 1)) + tuple((t, c, n) for t in (A, B) for c, n in ((1, 1), (2, 2)))
+        gather_last(NCH - 1)
+        passes2 = ((A, 0, 1), (B, 0, 1)) + tuple((t, c, n) for t in (A, B) for c, n in first_middle_last[1:])
         passes2 = passes2 + tuple((t, c, 2) for t in (C, L) for c in (0, 2))
         for i, (t, c, n) in enumerate(passes2):
             product(bank(0, i % SPANS), w2_q, w2_s, t, rq, rs, z[t], c, n)
+            if i == 0:
+                quantise(NCH - 1)
         for c, n in first_and_rest:
             for i, t in enumerate((A, B)):
                 scatter(spread2[i], idx2, z[t], g2, c, n)

@@ -27,7 +27,8 @@ BLOCKS = BANK // P
 SPANS = T // BANK
 A, B, C, L = 2, 1, 0, 3
 ORDER = (A, B, C, L)
-LAST_EDGES = (0, 128, 384, 768, 1280, 1792, 2048)
+LAST_EDGES = (0, 128, 512, 1024, 1280, 1536)
+SHARE = 448
 FLOPS = 2 * 2 * K * K * S
 
 
@@ -111,7 +112,7 @@ def tile_moe_mod_silu_kernel(
                 dst[:].rearrange("p (t m) -> p t m", t=PACK), src[:].rearrange("p (m t) -> p t m", t=PACK)
             )
         nc.vector.memset(spread1[0][:], 0.0)
-        for t in ORDER:
+        for t in (L,) + ORDER[:-1]:
             nc.sync.dma_start(res[t][:], xr_v[:, t, :])
         nc.sync.dma_start(idx2[:], offs2)
         nc.sync.dma_start(g2[:], gate2)
@@ -171,6 +172,12 @@ def tile_moe_mod_silu_kernel(
         for i, (t, c, n) in enumerate(passes1):
             product(bank(1, i % SPANS), w1_q, w1_s, t, gw, gs, y[t], c, n)
 
+        res_turned = held("res_turned", [P, 2 * BANK], F32)
+        for g in range(2):
+            acc = bank(1, (len(passes1) + g) % SPANS)
+            turn(acc, res[L][:, span(g)], True, True)
+            nc.scalar.copy(res_turned[:, span(g)], acc[:])
+
         spread2 = [held("spread2_0", [P, T], F32, "gw"), held("spread2_1", [P, T], F32)]
         nc.scalar.copy(spread2[0][:], zeros)
         nc.sync.dma_start(spread2[1][:], spread2[0][:])
@@ -189,6 +196,10 @@ def tile_moe_mod_silu_kernel(
             for g in range(SPANS):
                 turn(sums[g], window[:, span(g)], False, True)
                 nc.scalar.copy(r_turned[t][:, span(g)], sums[g][:])
+            if t == C:
+                res_banks = [bank(i % 2, g) for g in range(2)]
+                for g in range(2):
+                    turn(res_banks[g], res_turned[:, span(g)], True, True)
             for g in range(SPANS):
                 back = bank(1 - i % 2, g)
                 turn(back, r_turned[t][:, span(g)], True, True)
@@ -197,7 +208,12 @@ def tile_moe_mod_silu_kernel(
                 nc.scalar.activation(in_pair(c, t), r16[t][:].indirect(entries(idx2, c)), COPY)
         scatter(spread1[1], idx1, y[L], g1, 0, NCH)
         r_last = held("r_last", [P, T], F32, "spread1_0")
-        nc.vector.tensor_tensor(r_last[:], res[L][:], spread1[1][:], ADD)
+        for g in range(2):
+            nc.vector.tensor_tensor(r_last[:, span(g)], spread1[1][:, span(g)], res_banks[g][:], ADD)
+        beside = slice(2 * BANK, 2 * BANK + SHARE)
+        nc.gpsimd.tensor_tensor(r_last[:, beside], res[L][:, beside], spread1[1][:, beside], ADD)
+        rest = slice(2 * BANK + SHARE, T)
+        nc.vector.tensor_tensor(r_last[:, rest], res[L][:, rest], spread1[1][:, rest], ADD)
 
         def gather_last(c):
             nc.vector.tensor_copy(in_pair(c, L), r_last[:].indirect(entries(idx2, c)))
@@ -224,6 +240,11 @@ def tile_moe_mod_silu_kernel(
             product(bank(0, i % SPANS), w2_q, w2_s, t, rq, rs, z[t], c, n)
             if i == 0:
                 quantise(NCH - 1)
+        last_turned = held("last_turned", [P, (SPANS - 1) * BANK], F32)
+        for g in range(SPANS - 1):
+            acc = bank(0, (len(passes2) + g) % SPANS)
+            turn(acc, r_last[:, span(g)], True, True)
+            nc.scalar.copy(last_turned[:, span(g)], acc[:])
         for c, n in first_and_rest:
             for i, t in enumerate((A, B)):
                 scatter(spread2[i], idx2, z[t], g2, c, n)
@@ -244,9 +265,16 @@ def tile_moe_mod_silu_kernel(
                 done = held(f"done{t}_{g}", [P, BANK], F32, f"done{g}")
                 nc.scalar.copy(done[:], sums[g][:])
                 nc.sync.dma_start(out_v[:, t, span(g)], done[:])
+        beside_last = span(SPANS - 1)
+        last_banks = [bank(0, g) for g in range(SPANS - 1)]
+        for g in range(SPANS - 1):
+            turn(last_banks[g], last_turned[:, span(g)], True, True)
         scatter(spread2[1], idx2, z[L], g2, 0, NCH)
         done_last = held("done_last", [P, T], F32, f"turned{SPANS - 1}")
         for lo, hi in zip(LAST_EDGES, LAST_EDGES[1:]):
             part = slice(lo, hi)
-            nc.vector.tensor_tensor(done_last[:, part], r_last[:, part], spread2[1][:, part], ADD)
+            acc = last_banks[lo // BANK][:, lo % BANK : lo % BANK + hi - lo]
+            nc.vector.tensor_tensor(done_last[:, part], spread2[1][:, part], acc, ADD)
             nc.scalar.dma_start(out_v[:, L, part], done_last[:, part])
+        nc.gpsimd.tensor_tensor(done_last[:, beside_last], r_last[:, beside_last], spread2[1][:, beside_last], ADD)
+        nc.sync.dma_start(out_v[:, L, beside_last], done_last[:, beside_last])

@@ -1,7 +1,6 @@
 from contextlib import ExitStack
 
 import concourse.mybir as mybir
-from concourse.masks import make_identity
 
 F32 = mybir.dt.float32
 BF16 = mybir.dt.bfloat16
@@ -23,13 +22,10 @@ PACK = 4
 CH = 256
 NCH = S // CH
 BANK = 512
-BLOCKS = BANK // P
-SPANS = T // BANK
-A, B, C, L = 2, 1, 0, 3
-ORDER = (A, B, C, L)
-LAST_EDGES = (0, 128, 512, 1024, 1280, 1536)
-SHARE = 448
+BANKS = 8
 FLOPS = 2 * 2 * K * K * S
+V1, S1, S2, V2 = 0, 1, 2, 3
+SCALAR_PIECES = ((0, 384), (384, 768), (768, 1024))
 
 
 def tile_moe_mod_silu_kernel(
@@ -57,15 +53,11 @@ def tile_moe_mod_silu_kernel(
         g2 = held("g2", [P, S], F32)
         zero = held("zero", [P, 2], F32)
         res = [held(f"res{t}", [P, T], F32) for t in range(PACK)]
-        spread1 = [held("spread1_0", [P, T], F32)]
-        ident = held("ident", [P, P], F32)
         gw = held("gw", [P, S], U32)
         gs = held("gs", [P, S], U8)
         y = [held(f"y{t}", [P, S], F32) for t in range(PACK)]
         z = [held(f"z{t}", [P, S], F32) for t in range(PACK)]
-        shared = held("shared", [P, CH * (2 * PACK - 1)], BF16)
-        rows_last = shared[:, : CH * PACK]
-        pairs = [shared[:, CH * (PACK - 1) :]] + [held(f"pairs{c}", [P, CH * PACK], BF16)[:] for c in range(1, NCH - 1)]
+        rg = held("rg", [P, PACK, S], F32)
         rb = [held(f"rb{c}", [P, CH * PACK], BF16) for c in range(NCH)]
         rq = held("rq", [P, S], U32)
         rs = held("rs", [P, S], U8)
@@ -77,13 +69,8 @@ def tile_moe_mod_silu_kernel(
         def cols(c, n=1):
             return slice(c * CH, (c + n) * CH)
 
-        def entries(idx, c, n=1):
-            return idx[:, c * CH // 16 : (c + n) * CH // 16]
-
-        def in_pair(c, t):
-            if c == NCH - 1:
-                return rows_last[:, cols(t)]
-            return pairs[c].rearrange("p (u s e) -> p u s e", u=2, e=2)[:, t // 2, :, t % 2]
+        def entries(idx, part):
+            return idx[:, part.start // 16 : part.stop // 16]
 
         def load_scale_rows(scale_tile, rows):
             for q in range(4):
@@ -104,15 +91,16 @@ def tile_moe_mod_silu_kernel(
         nc.sync.dma_start(w2_raw[:], w2_words[0].rearrange("p n d -> p (n d)").bitcast(I32))
         load_scale_rows(w2s_raw, w2_scales)
         nc.sync.dma_start(g1[:, cols(1, NCH - 1)], gate1[:, cols(1, NCH - 1)])
-        make_identity(nc, ident[:])
         w2_q = held("w2_q", [P, K], I32)
         w2_s = held("w2_s", [P, K], U8)
         for dst, src in ((w2_q, w2_raw), (w2_s, w2s_raw)):
             nc.gpsimd.tensor_copy(
                 dst[:].rearrange("p (t m) -> p t m", t=PACK), src[:].rearrange("p (m t) -> p t m", t=PACK)
             )
-        nc.vector.memset(spread1[0][:], 0.0)
-        for t in (L,) + ORDER[:-1]:
+        spread = {V1: held("spread_v", [P, T], F32), S1: held("spread_s1", [P, T], F32)}
+        nc.vector.memset(spread[V1][:], 0.0)
+        nc.scalar.copy(spread[S1][:], zero[:, 1:2].to_broadcast([P, T]))
+        for t in (V1, S1, S2, V2):
             nc.sync.dma_start(res[t][:], xr_v[:, t, :])
         nc.sync.dma_start(idx2[:], offs2)
         nc.sync.dma_start(g2[:], gate2)
@@ -123,158 +111,78 @@ def tile_moe_mod_silu_kernel(
             nc.scalar.copy(
                 w1_dst[:, P // 2 * h : P // 2 * (h + 1)], w1_raw[h][:].rearrange("p j (m t) -> p m t j", t=PACK)
             )
-        zeros = zero[:, 1:2].to_broadcast([P, T])
-        spread1.append(held("spread1_1", [P, T], F32, "w1_raw1"))
-        nc.scalar.copy(spread1[1][:], zeros)
         nc.vector.quantize_mx(out=w1_q[:].bitcast(FP8X4), scales=w1_s[:], in_=w1_bf[:])
-        first_and_rest = ((0, 1), (1, NCH - 1))
         first_middle_last = ((0, 1), (1, NCH - 2), (NCH - 1, 1))
         for c, n in first_middle_last:
-            nc.vector.tensor_copy(gw[:, cols(c, n)], xw[:].bitcast(U32).indirect(entries(idx1, c, n)))
+            nc.vector.tensor_copy(gw[:, cols(c, n)], xw[:].bitcast(U32).indirect(entries(idx1, cols(c, n))))
+        spread[S2] = held("spread_s2", [P, T], F32, "xw")
+        nc.gpsimd.memset(spread[S2][:], 0.0)
+        spread[V2] = spread[V1]
 
-        def bank(half, g):
-            return psum.tile([P, BANK], F32, name=f"bank{half}_{g}")
+        def products(passes, wq, ws, codes, scales, dst):
+            for i, (t, c, n) in passes:
+                acc = psum.tile([P, BANK], F32, name=f"bank{i % BANKS}")
+                w_cols = slice(t * P, (t + 1) * P)
+                nc.tensor.matmul_mx(
+                    out=acc[:, : n * CH],
+                    lhsT=wq[:, w_cols].bitcast(FP8X4),
+                    lhsT_scale=ws[:, w_cols],
+                    rhs=codes[:, cols(c, n)].bitcast(FP8X4),
+                    rhs_scale=scales[:, cols(c, n)],
+                    start=True,
+                    stop=True,
+                )
+                nc.scalar.activation(dst[t][:, cols(c, n)], acc[:, : n * CH], SILU)
 
-        def product(acc, wq, ws, t, codes, scales, dst, c, n):
-            w_cols = slice(t * P, (t + 1) * P)
-            nc.tensor.matmul_mx(
-                out=acc[:, : n * CH],
-                lhsT=wq[:, w_cols].bitcast(FP8X4),
-                lhsT_scale=ws[:, w_cols],
-                rhs=codes[:, cols(c, n)].bitcast(FP8X4),
-                rhs_scale=scales[:, cols(c, n)],
-                start=True,
-                stop=True,
+        def on_vector(window, idx, part, left, right, op):
+            nc.vector.tensor_tensor(window[:].indirect(entries(idx, part)), left[:, part], right[:, part], op)
+
+        def on_scalar(window, idx, values):
+            for lo, hi in SCALAR_PIECES:
+                part = slice(lo, hi)
+                nc.scalar.activation(window[:].indirect(entries(idx, part)), values[:, part], COPY)
+
+        def in_place(tile, part, other, op):
+            nc.vector.tensor_tensor(tile[:, part], tile[:, part], other[:, part], op)
+
+        everything = slice(0, S)
+        tokens = slice(0, T)
+        passes1 = ((V1, 0, 1),) + tuple((S1, c, n) for c, n in first_middle_last)
+        passes1 = passes1 + tuple((V1, c, n) for c, n in first_middle_last[1:])
+        passes1 = passes1 + tuple((t, c, 2) for t in (S2, V2) for c in (0, 2))
+        products(enumerate(passes1), w1_q, w1_s, gw, gs, y)
+        on_vector(spread[V1], idx1, cols(0), y[V1], g1, MULT)
+        in_place(y[S1], everything, g1, MULT)
+        on_vector(spread[V1], idx1, cols(1, NCH - 1), y[V1], g1, MULT)
+        on_scalar(spread[S1], idx1, y[S1])
+        in_place(y[S2], everything, g1, MULT)
+        on_scalar(spread[S2], idx1, y[S2])
+        in_place(res[V1], tokens, spread[V1], ADD)
+        on_vector(spread[V2], idx1, everything, y[V2], g1, MULT)
+        for t in (S1, S2, V2):
+            in_place(res[t], tokens, spread[t], ADD)
+
+        for t in (V1, S1, S2):
+            nc.scalar.activation(rg[:, t, :], res[t][:].indirect(idx2[:]), COPY)
+        for c in range(NCH):
+            nc.scalar.activation(rg[:, V2, cols(c)], res[V2][:].indirect(entries(idx2, cols(c))), COPY)
+            nc.vector.tensor_copy(
+                rb[c][:].rearrange("p (s t) -> p s t", t=PACK), rg[:, :, cols(c)].rearrange("p t s -> p s t")
             )
-            nc.scalar.activation(dst[:, cols(c, n)], acc[:, : n * CH], SILU)
-
-        def scatter(window, idx, values, gate, c, n):
-            nc.vector.tensor_tensor(
-                window[:].indirect(entries(idx, c, n)), values[:, cols(c, n)], gate[:, cols(c, n)], MULT
-            )
-
-        def turn(acc, src, start, stop):
-            for b in range(BLOCKS):
-                blk = slice(b * P, (b + 1) * P)
-                nc.tensor.matmul(
-                    acc[:, blk],
-                    src[:, blk],
-                    ident[:],
-                    start=start and b == 0,
-                    stop=stop and b == BLOCKS - 1,
-                    is_transpose=True,
-                )
-
-        def span(g):
-            return slice(g * BANK, (g + 1) * BANK)
-
-        passes1 = tuple((A, c, n) for c, n in first_middle_last) + tuple((t, c, 2) for t in ORDER[1:] for c in (0, 2))
-        for i, (t, c, n) in enumerate(passes1):
-            product(bank(1, i % SPANS), w1_q, w1_s, t, gw, gs, y[t], c, n)
-
-        res_turned = held("res_turned", [P, 2 * BANK], F32)
-        for g in range(2):
-            acc = bank(1, (len(passes1) + g) % SPANS)
-            turn(acc, res[L][:, span(g)], True, True)
-            nc.scalar.copy(res_turned[:, span(g)], acc[:])
-
-        spread2 = [held("spread2_0", [P, T], F32, "gw"), held("spread2_1", [P, T], F32)]
-        nc.scalar.copy(spread2[0][:], zeros)
-        nc.sync.dma_start(spread2[1][:], spread2[0][:])
-
-        r_turned = {}
-        r16 = {}
-        for i, t in enumerate(ORDER[:-1]):
-            window = spread1[i % 2]
-            sums = [bank(i % 2, g) for g in range(SPANS)]
-            for g in range(SPANS):
-                turn(sums[g], res[t][:, span(g)], True, False)
-            for c, n in first_and_rest if t == A else ((0, NCH),):
-                scatter(window, idx1, y[t], g1, c, n)
-            r_turned[t] = held(f"r_turned{t}", [P, T], F32, f"r16_{A}" if t == B else None)
-            r16[t] = held(f"r16_{t}", [P, T], BF16)
-            for g in range(SPANS):
-                turn(sums[g], window[:, span(g)], False, True)
-                nc.scalar.copy(r_turned[t][:, span(g)], sums[g][:])
-            if t == C:
-                res_banks = [bank(i % 2, g) for g in range(2)]
-                for g in range(2):
-                    turn(res_banks[g], res_turned[:, span(g)], True, True)
-            for g in range(SPANS):
-                back = bank(1 - i % 2, g)
-                turn(back, r_turned[t][:, span(g)], True, True)
-                nc.scalar.copy(r16[t][:, span(g)], back[:])
-            for c in range(NCH):
-                nc.scalar.activation(in_pair(c, t), r16[t][:].indirect(entries(idx2, c)), COPY)
-        scatter(spread1[1], idx1, y[L], g1, 0, NCH)
-        r_last = held("r_last", [P, T], F32, "spread1_0")
-        for g in range(2):
-            nc.vector.tensor_tensor(r_last[:, span(g)], spread1[1][:, span(g)], res_banks[g][:], ADD)
-        beside = slice(2 * BANK, 2 * BANK + SHARE)
-        nc.gpsimd.tensor_tensor(r_last[:, beside], res[L][:, beside], spread1[1][:, beside], ADD)
-        rest = slice(2 * BANK + SHARE, T)
-        nc.vector.tensor_tensor(r_last[:, rest], res[L][:, rest], spread1[1][:, rest], ADD)
-
-        def gather_last(c):
-            nc.vector.tensor_copy(in_pair(c, L), r_last[:].indirect(entries(idx2, c)))
-
-        def quantise(c):
-            if c == NCH - 1:
-                nc.scalar.copy(
-                    rb[c][:].rearrange("p (s t) -> p s t", t=PACK), rows_last.rearrange("p (t s) -> p s t", t=PACK)
-                )
-            else:
-                nc.scalar.copy(
-                    rb[c][:].bitcast(U32).rearrange("p (s u) -> p s u", u=2),
-                    pairs[c].bitcast(U32).rearrange("p (u s) -> p s u", u=2),
-                )
             nc.vector.quantize_mx(out=rq[:, cols(c)].bitcast(FP8X4), scales=rs[:, cols(c)], in_=rb[c][:])
-
-        for c in range(NCH - 1):
-            gather_last(c)
-            quantise(c)
-        gather_last(NCH - 1)
-        passes2 = ((A, 0, 1), (B, 0, 1)) + tuple((t, c, n) for t in (A, B) for c, n in first_middle_last[1:])
-        passes2 = passes2 + tuple((t, c, 2) for t in (C, L) for c in (0, 2))
-        for i, (t, c, n) in enumerate(passes2):
-            product(bank(0, i % SPANS), w2_q, w2_s, t, rq, rs, z[t], c, n)
-            if i == 0:
-                quantise(NCH - 1)
-        last_turned = held("last_turned", [P, (SPANS - 1) * BANK], F32)
-        for g in range(SPANS - 1):
-            acc = bank(0, (len(passes2) + g) % SPANS)
-            turn(acc, r_last[:, span(g)], True, True)
-            nc.scalar.copy(last_turned[:, span(g)], acc[:])
-        for c, n in first_and_rest:
-            for i, t in enumerate((A, B)):
-                scatter(spread2[i], idx2, z[t], g2, c, n)
-        for i, t in enumerate(ORDER[:-1]):
-            window = spread2[i % 2]
-            if t == C:
-                scatter(window, idx2, z[t], g2, 0, NCH)
-            sums = [bank(1 - i % 2, g) for g in range(SPANS)]
-            for g in range(SPANS):
-                turn(sums[g], r_turned[t][:, span(g)], True, False)
-            turned = [held(f"turned{t}_{g}", [P, BANK], F32, f"turned{g}") for g in range(SPANS)]
-            for g in range(SPANS):
-                there = bank(i % 2, g)
-                turn(there, window[:, span(g)], True, True)
-                nc.scalar.copy(turned[g][:], there[:])
-            for g in range(SPANS):
-                turn(sums[g], turned[g][:], False, True)
-                done = held(f"done{t}_{g}", [P, BANK], F32, f"done{g}")
-                nc.scalar.copy(done[:], sums[g][:])
-                nc.sync.dma_start(out_v[:, t, span(g)], done[:])
-        beside_last = span(SPANS - 1)
-        last_banks = [bank(0, g) for g in range(SPANS - 1)]
-        for g in range(SPANS - 1):
-            turn(last_banks[g], last_turned[:, span(g)], True, True)
-        scatter(spread2[1], idx2, z[L], g2, 0, NCH)
-        done_last = held("done_last", [P, T], F32, f"turned{SPANS - 1}")
-        for lo, hi in zip(LAST_EDGES, LAST_EDGES[1:]):
-            part = slice(lo, hi)
-            acc = last_banks[lo // BANK][:, lo % BANK : lo % BANK + hi - lo]
-            nc.vector.tensor_tensor(done_last[:, part], spread2[1][:, part], acc, ADD)
-            nc.scalar.dma_start(out_v[:, L, part], done_last[:, part])
-        nc.gpsimd.tensor_tensor(done_last[:, beside_last], r_last[:, beside_last], spread2[1][:, beside_last], ADD)
-        nc.sync.dma_start(out_v[:, L, beside_last], done_last[:, beside_last])
+        passes2 = tuple((t, c, 1) for c in range(NCH) for t in (S1, V1))
+        passes2 = passes2 + tuple((t, c, 2) for t in (S2, V2) for c in (0, 2))
+        products(enumerate(passes2), w2_q, w2_s, rq, rs, z)
+        for part in (cols(0, NCH - 1), cols(NCH - 1)):
+            in_place(z[S1], part, g2, MULT)
+            in_place(z[S1], part, rg[:, S1, :], ADD)
+        in_place(z[V1], everything, g2, MULT)
+        in_place(z[S2], everything, g2, MULT)
+        in_place(z[S2], everything, rg[:, S2, :], ADD)
+        for t in (S1, S2):
+            on_scalar(res[t], idx2, z[t])
+        on_vector(res[V1], idx2, everything, z[V1], rg[:, V1, :], ADD)
+        in_place(z[V2], everything, g2, MULT)
+        on_vector(res[V2], idx2, everything, z[V2], rg[:, V2, :], ADD)
+        for t in (S1, V1, S2, V2):
+            nc.sync.dma_start(out_v[:, t, :], res[t][:])

@@ -25,7 +25,8 @@ BANK = 512
 BANKS = 8
 FLOPS = 2 * 2 * K * K * S
 V1, S1, S2, V2 = 0, 1, 2, 3
-SCALAR_PIECES = ((0, 384), (384, 768), (768, 1024))
+WIDE = 384
+SCALAR_PIECES = ((0, CH), (CH, CH + WIDE), (CH + WIDE, S))
 
 
 def tile_moe_mod_silu_kernel(
@@ -99,7 +100,7 @@ def tile_moe_mod_silu_kernel(
             )
         spread = {V1: held("spread_v", [P, T], F32), S1: held("spread_s1", [P, T], F32)}
         nc.vector.memset(spread[V1][:], 0.0)
-        nc.scalar.copy(spread[S1][:], zero[:, 1:2].to_broadcast([P, T]))
+        nc.gpsimd.memset(spread[S1][:], 0.0)
         for t in (V1, S1, S2, V2):
             nc.sync.dma_start(res[t][:], xr_v[:, t, :])
         nc.sync.dma_start(idx2[:], offs2)
@@ -112,8 +113,7 @@ def tile_moe_mod_silu_kernel(
                 w1_dst[:, P // 2 * h : P // 2 * (h + 1)], w1_raw[h][:].rearrange("p j (m t) -> p m t j", t=PACK)
             )
         nc.vector.quantize_mx(out=w1_q[:].bitcast(FP8X4), scales=w1_s[:], in_=w1_bf[:])
-        first_middle_last = ((0, 1), (1, NCH - 2), (NCH - 1, 1))
-        for c, n in first_middle_last:
+        for c, n in ((0, 1), (1, NCH - 1)):
             nc.vector.tensor_copy(gw[:, cols(c, n)], xw[:].bitcast(U32).indirect(entries(idx1, cols(c, n))))
         spread[S2] = held("spread_s2", [P, T], F32, "xw")
         nc.gpsimd.memset(spread[S2][:], 0.0)
@@ -147,9 +147,8 @@ def tile_moe_mod_silu_kernel(
 
         everything = slice(0, S)
         tokens = slice(0, T)
-        passes1 = ((V1, 0, 1),) + tuple((S1, c, n) for c, n in first_middle_last)
-        passes1 = passes1 + tuple((V1, c, n) for c, n in first_middle_last[1:])
-        passes1 = passes1 + tuple((t, c, 2) for t in (S2, V2) for c in (0, 2))
+        passes1 = tuple((t, 0, 1) for t in (V1, S1, S2, V2))
+        passes1 = passes1 + tuple((t, c, n) for t in (S1, V1, S2, V2) for c, n in ((1, 2), (3, 1)))
         products(enumerate(passes1), w1_q, w1_s, gw, gs, y)
         on_vector(spread[V1], idx1, cols(0), y[V1], g1, MULT)
         in_place(y[S1], everything, g1, MULT)
@@ -164,25 +163,25 @@ def tile_moe_mod_silu_kernel(
 
         for t in (V1, S1, S2):
             nc.scalar.activation(rg[:, t, :], res[t][:].indirect(idx2[:]), COPY)
+        for c in range(2):
+            nc.vector.tensor_copy(rg[:, V2, cols(c)], res[V2][:].indirect(entries(idx2, cols(c))))
+        nc.scalar.activation(rg[:, V2, cols(2, 2)], res[V2][:].indirect(entries(idx2, cols(2, 2))), COPY)
         for c in range(NCH):
-            nc.scalar.activation(rg[:, V2, cols(c)], res[V2][:].indirect(entries(idx2, cols(c))), COPY)
-            nc.vector.tensor_copy(
-                rb[c][:].rearrange("p (s t) -> p s t", t=PACK), rg[:, :, cols(c)].rearrange("p t s -> p s t")
-            )
+            cast = nc.scalar.copy if c == 2 else nc.vector.tensor_copy
+            cast(rb[c][:].rearrange("p (s t) -> p s t", t=PACK), rg[:, :, cols(c)].rearrange("p t s -> p s t"))
             nc.vector.quantize_mx(out=rq[:, cols(c)].bitcast(FP8X4), scales=rs[:, cols(c)], in_=rb[c][:])
-        passes2 = tuple((t, c, 1) for c in range(NCH) for t in (S1, V1))
-        passes2 = passes2 + tuple((t, c, 2) for t in (S2, V2) for c in (0, 2))
+        passes2 = tuple((t, c, 2) for c in (0, 2) for t in (S1, S2))
+        passes2 = passes2 + tuple((t, c, 2) for t in (V1, V2) for c in (0, 2))
         products(enumerate(passes2), w2_q, w2_s, rq, rs, z)
-        for part in (cols(0, NCH - 1), cols(NCH - 1)):
-            in_place(z[S1], part, g2, MULT)
-            in_place(z[S1], part, rg[:, S1, :], ADD)
-        in_place(z[V1], everything, g2, MULT)
-        in_place(z[S2], everything, g2, MULT)
-        in_place(z[S2], everything, rg[:, S2, :], ADD)
+        for t, c in ((S1, 0), (S2, 0), (S1, 2), (S2, 2)):
+            in_place(z[t], cols(c, 2), g2, MULT)
+        for t in (S1, S2):
+            in_place(z[t], everything, rg[:, t, :], ADD)
+        for t in (V1, V2):
+            in_place(z[t], everything, g2, MULT)
         for t in (S1, S2):
             on_scalar(res[t], idx2, z[t])
-        on_vector(res[V1], idx2, everything, z[V1], rg[:, V1, :], ADD)
-        in_place(z[V2], everything, g2, MULT)
-        on_vector(res[V2], idx2, everything, z[V2], rg[:, V2, :], ADD)
+        for t in (V1, V2):
+            on_vector(res[t], idx2, everything, z[t], rg[:, t, :], ADD)
         for t in (S1, V1, S2, V2):
             nc.sync.dma_start(out_v[:, t, :], res[t][:])

@@ -24,7 +24,8 @@ NCH = S // CH
 BANK = 512
 BANKS = 8
 FLOPS = 2 * 2 * K * K * S
-V1, S1, S2, V2 = 0, 1, 2, 3
+V1, S1, V2, S2 = 0, 1, 2, 3
+SHARE = 768
 WIDE = 384
 SCALAR_PIECES = ((0, CH), (CH, CH + WIDE), (CH + WIDE, S))
 
@@ -53,12 +54,13 @@ def tile_moe_mod_silu_kernel(
         g1 = held("g1", [P, S], F32)
         g2 = held("g2", [P, S], F32)
         zero = held("zero", [P, 2], F32)
-        res = [held(f"res{t}", [P, T], F32) for t in range(PACK)]
-        gw = held("gw", [P, S], U32)
+        rg_flat = held("rg", [P, PACK * S], F32)
+        rg = rg_flat[:].rearrange("p (t s) -> p t s", t=PACK)
+        res = {t: held(f"res{t}", [P, T], F32)[:] for t in (V1, S1, V2)}
+        res[S2] = rg_flat[:, V2 * S :]
         gs = held("gs", [P, S], U8)
         y = [held(f"y{t}", [P, S], F32) for t in range(PACK)]
         z = [held(f"z{t}", [P, S], F32) for t in range(PACK)]
-        rg = held("rg", [P, PACK, S], F32)
         rb = [held(f"rb{c}", [P, CH * PACK], BF16) for c in range(NCH)]
         rq = held("rq", [P, S], U32)
         rs = held("rs", [P, S], U8)
@@ -99,10 +101,13 @@ def tile_moe_mod_silu_kernel(
                 dst[:].rearrange("p (t m) -> p t m", t=PACK), src[:].rearrange("p (m t) -> p t m", t=PACK)
             )
         spread = {V1: held("spread_v", [P, T], F32), S1: held("spread_s1", [P, T], F32)}
-        nc.vector.memset(spread[V1][:], 0.0)
-        nc.gpsimd.memset(spread[S1][:], 0.0)
-        for t in (V1, S1, S2, V2):
-            nc.sync.dma_start(res[t][:], xr_v[:, t, :])
+        spread[V2] = held("spread_v2", [P, T], F32)
+        for t in (V1, S1):
+            nc.gpsimd.memset(spread[t][:], 0.0)
+        nc.scalar.copy(spread[V2][:, :S], zero[:, 1:2].to_broadcast([P, S]))
+        nc.gpsimd.memset(spread[V2][:, S:], 0.0)
+        for t in (V1, S1, V2, S2):
+            nc.sync.dma_start(res[t], xr_v[:, t, :])
         nc.sync.dma_start(idx2[:], offs2)
         nc.sync.dma_start(g2[:], gate2)
 
@@ -113,11 +118,11 @@ def tile_moe_mod_silu_kernel(
                 w1_dst[:, P // 2 * h : P // 2 * (h + 1)], w1_raw[h][:].rearrange("p j (m t) -> p m t j", t=PACK)
             )
         nc.vector.quantize_mx(out=w1_q[:].bitcast(FP8X4), scales=w1_s[:], in_=w1_bf[:])
+        gw = held("gw", [P, S], U32, "w1_bf")
         for c, n in ((0, 1), (1, NCH - 1)):
             nc.vector.tensor_copy(gw[:, cols(c, n)], xw[:].bitcast(U32).indirect(entries(idx1, cols(c, n))))
         spread[S2] = held("spread_s2", [P, T], F32, "xw")
         nc.gpsimd.memset(spread[S2][:], 0.0)
-        spread[V2] = spread[V1]
 
         def products(passes, wq, ws, codes, scales, dst):
             for i, (t, c, n) in passes:
@@ -146,42 +151,55 @@ def tile_moe_mod_silu_kernel(
             nc.vector.tensor_tensor(tile[:, part], tile[:, part], other[:, part], op)
 
         everything = slice(0, S)
-        tokens = slice(0, T)
         passes1 = tuple((t, 0, 1) for t in (V1, S1, S2, V2))
         passes1 = passes1 + tuple((t, c, n) for t in (S1, V1, S2, V2) for c, n in ((1, 2), (3, 1)))
         products(enumerate(passes1), w1_q, w1_s, gw, gs, y)
         on_vector(spread[V1], idx1, cols(0), y[V1], g1, MULT)
         in_place(y[S1], everything, g1, MULT)
-        on_vector(spread[V1], idx1, cols(1, NCH - 1), y[V1], g1, MULT)
+        rest = cols(1, NCH - 1)
+        gated_v1 = held("gated_v1", [P, S], F32)
+        nc.vector.tensor_tensor(gated_v1[:, rest], y[V1][:, rest], g1[:, rest], MULT)
+        nc.vector.tensor_copy(spread[V1][:].indirect(entries(idx1, rest)), gated_v1[:, rest])
         on_scalar(spread[S1], idx1, y[S1])
-        in_place(y[S2], everything, g1, MULT)
-        on_scalar(spread[S2], idx1, y[S2])
-        in_place(res[V1], tokens, spread[V1], ADD)
-        on_vector(spread[V2], idx1, everything, y[V2], g1, MULT)
-        for t in (S1, S2, V2):
-            in_place(res[t], tokens, spread[t], ADD)
+        nc.gpsimd.tensor_tensor(y[V1][:], y[S2][:], g1[:], MULT)
+        on_scalar(spread[S2], idx1, y[V1])
+        r = {S1: held("r_s1", [P, T], F32)}
+        nc.gpsimd.tensor_tensor(r[S1][:, S:], y[V2][:], g1[:], MULT)
+        nc.vector.tensor_copy(spread[V2][:].indirect(idx1[:]), r[S1][:, S:])
+        r[V1] = held("r_v1", [P, T], F32)
+        nc.gpsimd.tensor_tensor(r[V1][:], res[V1], spread[V1][:], ADD)
+        nc.gpsimd.tensor_tensor(r[S1][:, :SHARE], res[S1][:, :SHARE], spread[S1][:, :SHARE], ADD)
+        nc.vector.tensor_tensor(r[S1][:, SHARE:], res[S1][:, SHARE:], spread[S1][:, SHARE:], ADD)
+        r[V2] = held("r_v2", [P, T], F32, "spread_v")
+        r[S2] = held("r_s2", [P, T], F32, f"res{S1}")
+        for t in (V2, S2):
+            nc.vector.tensor_tensor(r[t][:], res[t], spread[t][:], ADD)
 
-        for t in (V1, S1, S2):
-            nc.scalar.activation(rg[:, t, :], res[t][:].indirect(idx2[:]), COPY)
-        for c in range(2):
-            nc.vector.tensor_copy(rg[:, V2, cols(c)], res[V2][:].indirect(entries(idx2, cols(c))))
-        nc.scalar.activation(rg[:, V2, cols(2, 2)], res[V2][:].indirect(entries(idx2, cols(2, 2))), COPY)
+        for t in (V1, S1):
+            nc.scalar.activation(rg[:, t, :], r[t][:].indirect(idx2[:]), COPY)
+        nc.vector.tensor_copy(rg[:, V2, :], r[V2][:].indirect(idx2[:]))
+        for c, n in ((0, 1), (1, 1), (2, 2)):
+            nc.scalar.activation(rg[:, S2, cols(c, n)], r[S2][:].indirect(entries(idx2, cols(c, n))), COPY)
         for c in range(NCH):
-            cast = nc.scalar.copy if c == 2 else nc.vector.tensor_copy
-            cast(rb[c][:].rearrange("p (s t) -> p s t", t=PACK), rg[:, :, cols(c)].rearrange("p t s -> p s t"))
+            nc.vector.tensor_copy(
+                rb[c][:].rearrange("p (s t) -> p s t", t=PACK), rg[:, :, cols(c)].rearrange("p t s -> p s t")
+            )
             nc.vector.quantize_mx(out=rq[:, cols(c)].bitcast(FP8X4), scales=rs[:, cols(c)], in_=rb[c][:])
         passes2 = tuple((t, c, 2) for c in (0, 2) for t in (S1, S2))
         passes2 = passes2 + tuple((t, c, 2) for t in (V1, V2) for c in (0, 2))
         products(enumerate(passes2), w2_q, w2_s, rq, rs, z)
-        for t, c in ((S1, 0), (S2, 0), (S1, 2), (S2, 2)):
-            in_place(z[t], cols(c, 2), g2, MULT)
-        for t in (S1, S2):
-            in_place(z[t], everything, rg[:, t, :], ADD)
+        for c in (0, 2):
+            for t in (S1, S2):
+                in_place(z[t], cols(c, 2), g2, MULT)
+            for t in (S1, S2):
+                in_place(z[t], cols(c, 2), rg[:, t, :], ADD)
         for t in (V1, V2):
             in_place(z[t], everything, g2, MULT)
         for t in (S1, S2):
-            on_scalar(res[t], idx2, z[t])
+            on_scalar(r[t], idx2, z[t])
         for t in (V1, V2):
-            on_vector(res[t], idx2, everything, z[t], rg[:, t, :], ADD)
-        for t in (S1, V1, S2, V2):
-            nc.sync.dma_start(out_v[:, t, :], res[t][:])
+            on_vector(r[t], idx2, everything, z[t], rg[:, t, :], ADD)
+        for t in (S1, S2):
+            nc.scalar.dma_start(out_v[:, t, :], r[t][:])
+        for t in (V1, V2):
+            nc.sync.dma_start(out_v[:, t, :], r[t][:])

@@ -1,6 +1,7 @@
 from contextlib import ExitStack
 
 import concourse.mybir as mybir
+from concourse.masks import make_identity
 
 F32 = mybir.dt.float32
 BF16 = mybir.dt.bfloat16
@@ -22,12 +23,14 @@ PACK = 4
 CH = 256
 NCH = S // CH
 BANK = 512
-BANKS = 8
+BANKS = 6
+HALF = S // 2
 FLOPS = 2 * 2 * K * K * S
 V1, S1, V2, S2 = 0, 1, 2, 3
 SHARE = 768
 WIDE = 384
-SCALAR_PIECES = ((0, CH), (CH, CH + WIDE), (CH + WIDE, S))
+SCALAR_PIECES = ((0, WIDE), (WIDE, 2 * WIDE), (2 * WIDE, S))
+LAST_WIDE = ((0, CH), (CH, CH + WIDE), (CH + WIDE, S))
 
 
 def tile_moe_mod_silu_kernel(
@@ -53,11 +56,13 @@ def tile_moe_mod_silu_kernel(
         w2s_raw = held("w2s_raw", [P, K], U8)
         g1 = held("g1", [P, S], F32)
         g2 = held("g2", [P, S], F32)
+        g2_rows = held("g2_rows", [P, 2, PACK], F32)
+        ident = held("ident", [P, P], F32)
         zero = held("zero", [P, 2], F32)
         rg_flat = held("rg", [P, PACK * S], F32)
         rg = rg_flat[:].rearrange("p (t s) -> p t s", t=PACK)
         res = {t: held(f"res{t}", [P, T], F32)[:] for t in (V1, S1, V2)}
-        res[S2] = rg_flat[:, V2 * S :]
+        res[S2] = rg_flat[:, S1 * S + S // 2 : S2 * S + S // 2]
         gs = held("gs", [P, S], U8)
         y = [held(f"y{t}", [P, S], F32) for t in range(PACK)]
         z = [held(f"z{t}", [P, S], F32) for t in range(PACK)]
@@ -106,10 +111,12 @@ def tile_moe_mod_silu_kernel(
             nc.gpsimd.memset(spread[t][:], 0.0)
         nc.scalar.copy(spread[V2][:, :S], zero[:, 1:2].to_broadcast([P, S]))
         nc.gpsimd.memset(spread[V2][:, S:], 0.0)
+        make_identity(nc, ident[:])
         for t in (V1, S1, V2, S2):
             nc.sync.dma_start(res[t], xr_v[:, t, :])
         nc.sync.dma_start(idx2[:], offs2)
-        nc.sync.dma_start(g2[:], gate2)
+        nc.sync.dma_start(g2[:, HALF:], gate2[:, HALF:])
+        nc.sync.dma_start(g2_rows[:], gate2[0].rearrange("(h j i) -> j h i", h=2, i=PACK))
 
         nc.vector.tensor_copy(gs[:], xs[:].indirect(idx1[:]))
         w1_dst = w1_bf[:].rearrange("p (t m j) -> p m t j", t=PACK, j=PACK)
@@ -126,7 +133,7 @@ def tile_moe_mod_silu_kernel(
 
         def products(passes, wq, ws, codes, scales, dst):
             for i, (t, c, n) in passes:
-                acc = psum.tile([P, BANK], F32, name=f"bank{i % BANKS}")
+                acc = psum.tile([P, BANK], F32, name=f"bank{i}")
                 w_cols = slice(t * P, (t + 1) * P)
                 nc.tensor.matmul_mx(
                     out=acc[:, : n * CH],
@@ -142,8 +149,8 @@ def tile_moe_mod_silu_kernel(
         def on_vector(window, idx, part, left, right, op):
             nc.vector.tensor_tensor(window[:].indirect(entries(idx, part)), left[:, part], right[:, part], op)
 
-        def on_scalar(window, idx, values):
-            for lo, hi in SCALAR_PIECES:
+        def on_scalar(window, idx, values, pieces=SCALAR_PIECES):
+            for lo, hi in pieces:
                 part = slice(lo, hi)
                 nc.scalar.activation(window[:].indirect(entries(idx, part)), values[:, part], COPY)
 
@@ -153,7 +160,7 @@ def tile_moe_mod_silu_kernel(
         everything = slice(0, S)
         passes1 = tuple((t, 0, 1) for t in (V1, S1, S2, V2))
         passes1 = passes1 + tuple((t, c, n) for t in (S1, V1, S2, V2) for c, n in ((1, 2), (3, 1)))
-        products(enumerate(passes1), w1_q, w1_s, gw, gs, y)
+        products(((i % BANKS, one) for i, one in enumerate(passes1)), w1_q, w1_s, gw, gs, y)
         on_vector(spread[V1], idx1, cols(0), y[V1], g1, MULT)
         in_place(y[S1], everything, g1, MULT)
         rest = cols(1, NCH - 1)
@@ -175,30 +182,57 @@ def tile_moe_mod_silu_kernel(
         for t in (V2, S2):
             nc.vector.tensor_tensor(r[t][:], res[t], spread[t][:], ADD)
 
-        for t in (V1, S1):
-            nc.scalar.activation(rg[:, t, :], r[t][:].indirect(idx2[:]), COPY)
-        nc.vector.tensor_copy(rg[:, V2, :], r[V2][:].indirect(idx2[:]))
-        for c, n in ((0, 1), (1, 1), (2, 2)):
-            nc.scalar.activation(rg[:, S2, cols(c, n)], r[S2][:].indirect(entries(idx2, cols(c, n))), COPY)
-        for c in range(NCH):
-            nc.vector.tensor_copy(
-                rb[c][:].rearrange("p (s t) -> p s t", t=PACK), rg[:, :, cols(c)].rearrange("p t s -> p s t")
-            )
-            nc.vector.quantize_mx(out=rq[:, cols(c)].bitcast(FP8X4), scales=rs[:, cols(c)], in_=rb[c][:])
-        passes2 = tuple((t, c, 2) for c in (0, 2) for t in (S1, S2))
-        passes2 = passes2 + tuple((t, c, 2) for t in (V1, V2) for c in (0, 2))
-        products(enumerate(passes2), w2_q, w2_s, rq, rs, z)
-        for c in (0, 2):
+        halves = (cols(0, 2), cols(2, 2))
+        nc.scalar.activation(rg[:, V1, :], r[V1][:].indirect(idx2[:]), COPY)
+        for h, half in enumerate(halves):
             for t in (S1, S2):
-                in_place(z[t], cols(c, 2), g2, MULT)
-            for t in (S1, S2):
-                in_place(z[t], cols(c, 2), rg[:, t, :], ADD)
-        for t in (V1, V2):
-            in_place(z[t], everything, g2, MULT)
-        for t in (S1, S2):
-            on_scalar(r[t], idx2, z[t])
-        for t in (V1, V2):
-            on_vector(r[t], idx2, everything, z[t], rg[:, t, :], ADD)
+                nc.scalar.activation(rg[:, t, half], r[t][:].indirect(entries(idx2, half)), COPY)
+            nc.vector.tensor_copy(rg[:, V2, half], r[V2][:].indirect(entries(idx2, half)))
+            for c in (2 * h, 2 * h + 1):
+                cast = nc.scalar.copy if c == NCH - 1 else nc.vector.tensor_copy
+                cast(
+                    rb[c][:].rearrange("p (s i t) -> p s t i", i=4, t=PACK),
+                    rg[:, :, cols(c)].rearrange("p t (s i) -> p s t i", i=4),
+                )
+                nc.vector.quantize_mx(out=rq[:, cols(c)].bitcast(FP8X4), scales=rs[:, cols(c)], in_=rb[c][:])
+        passes2 = tuple((t, c, 2) for pair in ((S1, V1), (S2, V2)) for c in (0, 2) for t in pair)
+        products(((i % BANKS, one) for i, one in enumerate(passes2)), w2_q, w2_s, rq, rs, z)
+        g2_banks = [psum.tile([P, BANK], F32, name=f"g2_bank{h}") for h in range(2)]
+        for h in range(2):
+            for i in range(PACK):
+                nc.tensor.transpose(
+                    g2_banks[h][:, i * P : (i + 1) * P], g2_rows[:, h, i : i + 1].to_broadcast([P, P]), ident[:]
+                )
+
+        def gate_on_vector(t, h):
+            values = z[t][:, halves[h]].rearrange("p (j i) -> p j i", i=PACK)
+            nc.vector.tensor_tensor(values, values, g2_banks[h][:].rearrange("p (i j) -> p j i", i=PACK), MULT)
+
+        def on_gpsimd(t, part, other, op):
+            nc.gpsimd.tensor_tensor(z[t][:, part], z[t][:, part], other[:, part], op)
+
+        def copy_on_vector(t, part):
+            nc.vector.tensor_copy(r[t][:].indirect(entries(idx2, part)), z[t][:, part])
+
+        for h in range(2):
+            for t in (S1, V1):
+                gate_on_vector(t, h)
+        for t in (S2, V2):
+            gate_on_vector(t, 0)
+        for half in halves:
+            for t in (S1, V1):
+                on_gpsimd(t, half, rg[:, t, :], ADD)
+        on_scalar(r[S1], idx2, z[S1])
+        for half in halves:
+            copy_on_vector(V1, half)
+        for t in (S2, V2):
+            on_gpsimd(t, halves[0], rg[:, t, :], ADD)
+        for t in (S2, V2):
+            on_gpsimd(t, halves[1], g2, MULT)
+            on_gpsimd(t, halves[1], rg[:, t, :], ADD)
+        on_scalar(r[S2], idx2, z[S2], LAST_WIDE)
+        for half in halves:
+            copy_on_vector(V2, half)
         for t in (S1, S2):
             nc.scalar.dma_start(out_v[:, t, :], r[t][:])
         for t in (V1, V2):

@@ -30,7 +30,7 @@ V1, S1, V2, S2 = 0, 1, 2, 3
 SHARE = 768
 WIDE = 384
 SCALAR_PIECES = ((0, WIDE), (WIDE, 2 * WIDE), (2 * WIDE, S))
-LAST_WIDE = ((0, CH), (CH, CH + WIDE), (CH + WIDE, S))
+CHUNKS = tuple((c * CH, (c + 1) * CH) for c in range(NCH))
 
 
 def tile_moe_mod_silu_kernel(
@@ -62,7 +62,7 @@ def tile_moe_mod_silu_kernel(
         rg_flat = held("rg", [P, PACK * S], F32)
         rg = rg_flat[:].rearrange("p (t s) -> p t s", t=PACK)
         res = {t: held(f"res{t}", [P, T], F32)[:] for t in (V1, S1, V2)}
-        res[S2] = rg_flat[:, S1 * S + S // 2 : S2 * S + S // 2]
+        res[S2] = rg_flat[:, V2 * S :]
         gs = held("gs", [P, S], U8)
         y = [held(f"y{t}", [P, S], F32) for t in range(PACK)]
         z = [held(f"z{t}", [P, S], F32) for t in range(PACK)]
@@ -183,11 +183,11 @@ def tile_moe_mod_silu_kernel(
             nc.vector.tensor_tensor(r[t][:], res[t], spread[t][:], ADD)
 
         halves = (cols(0, 2), cols(2, 2))
-        nc.scalar.activation(rg[:, V1, :], r[V1][:].indirect(idx2[:]), COPY)
+        for t in (V1, S1):
+            nc.scalar.activation(rg[:, t, :], r[t][:].indirect(idx2[:]), COPY)
+        nc.vector.tensor_copy(rg[:, V2, :], r[V2][:].indirect(idx2[:]))
         for h, half in enumerate(halves):
-            for t in (S1, S2):
-                nc.scalar.activation(rg[:, t, half], r[t][:].indirect(entries(idx2, half)), COPY)
-            nc.vector.tensor_copy(rg[:, V2, half], r[V2][:].indirect(entries(idx2, half)))
+            nc.scalar.activation(rg[:, S2, half], r[S2][:].indirect(entries(idx2, half)), COPY)
             for c in (2 * h, 2 * h + 1):
                 cast = nc.scalar.copy if c == NCH - 1 else nc.vector.tensor_copy
                 cast(
@@ -195,8 +195,9 @@ def tile_moe_mod_silu_kernel(
                     rg[:, :, cols(c)].rearrange("p t (s i) -> p s t i", i=4),
                 )
                 nc.vector.quantize_mx(out=rq[:, cols(c)].bitcast(FP8X4), scales=rs[:, cols(c)], in_=rb[c][:])
-        passes2 = tuple((t, c, 2) for pair in ((S1, V1), (S2, V2)) for c in (0, 2) for t in pair)
-        products(((i % BANKS, one) for i, one in enumerate(passes2)), w2_q, w2_s, rq, rs, z)
+        needed = ((V1, 0), (S1, 0), (S2, 0), (S1, 1), (V1, 1), (V2, 0), (S2, 1), (V2, 1))
+        passes2 = ((V1, 0, 1), (V1, 1, 1)) + tuple((t, 2 * h, 2) for t, h in needed[1:])
+        products(zip((0, 5, 1, 2, 3, 4, 3, 5, 0), passes2), w2_q, w2_s, rq, rs, z)
         g2_banks = [psum.tile([P, BANK], F32, name=f"g2_bank{h}") for h in range(2)]
         for h in range(2):
             for i in range(PACK):
@@ -214,23 +215,20 @@ def tile_moe_mod_silu_kernel(
         def copy_on_vector(t, part):
             nc.vector.tensor_copy(r[t][:].indirect(entries(idx2, part)), z[t][:, part])
 
-        for h in range(2):
-            for t in (S1, V1):
-                gate_on_vector(t, h)
-        for t in (S2, V2):
-            gate_on_vector(t, 0)
-        for half in halves:
-            for t in (S1, V1):
-                on_gpsimd(t, half, rg[:, t, :], ADD)
+        for t, h in needed[:-2]:
+            gate_on_vector(t, h)
+        for t, h in needed[:-3]:
+            on_gpsimd(t, halves[h], rg[:, t, :], ADD)
         on_scalar(r[S1], idx2, z[S1])
-        for half in halves:
-            copy_on_vector(V1, half)
-        for t in (S2, V2):
-            on_gpsimd(t, halves[0], rg[:, t, :], ADD)
-        for t in (S2, V2):
-            on_gpsimd(t, halves[1], g2, MULT)
-            on_gpsimd(t, halves[1], rg[:, t, :], ADD)
-        on_scalar(r[S2], idx2, z[S2], LAST_WIDE)
+        for part in (cols(0), cols(1), halves[1]):
+            copy_on_vector(V1, part)
+        between = rg[:, V1, halves[1]]
+        nc.gpsimd.tensor_tensor(between, z[S2][:, halves[1]], g2[:, halves[1]], MULT)
+        on_gpsimd(V2, halves[0], rg[:, V2, :], ADD)
+        nc.gpsimd.tensor_tensor(z[S2][:, halves[1]], between, rg[:, S2, halves[1]], ADD)
+        on_gpsimd(V2, halves[1], g2, MULT)
+        on_gpsimd(V2, halves[1], rg[:, V2, :], ADD)
+        on_scalar(r[S2], idx2, z[S2], CHUNKS)
         for half in halves:
             copy_on_vector(V2, half)
         for t in (S1, S2):

@@ -27,10 +27,8 @@ BANKS = 6
 HALF = S // 2
 FLOPS = 2 * 2 * K * K * S
 V1, S1, V2, S2 = 0, 1, 2, 3
-SHARE = 768
 WIDE = 384
 SCALAR_PIECES = ((0, WIDE), (WIDE, 2 * WIDE), (2 * WIDE, S))
-CHUNKS = tuple((c * CH, (c + 1) * CH) for c in range(NCH))
 
 
 def tile_moe_mod_silu_kernel(
@@ -99,12 +97,16 @@ def tile_moe_mod_silu_kernel(
         nc.sync.dma_start(w2_raw[:], w2_words[0].rearrange("p n d -> p (n d)").bitcast(I32))
         load_scale_rows(w2s_raw, w2_scales)
         nc.sync.dma_start(g1[:, cols(1, NCH - 1)], gate1[:, cols(1, NCH - 1)])
-        w2_q = held("w2_q", [P, K], I32)
-        w2_s = held("w2_s", [P, K], U8)
-        for dst, src in ((w2_q, w2_raw), (w2_s, w2s_raw)):
+
+        def to_planes(dst, src):
             nc.gpsimd.tensor_copy(
                 dst[:].rearrange("p (t m) -> p t m", t=PACK), src[:].rearrange("p (m t) -> p t m", t=PACK)
             )
+
+        w2_q = held("w2_q", [P, K], I32)
+        w2_s = held("w2_s", [P, K], U8)
+        to_planes(w2_q, w2_raw)
+        to_planes(w2_s, w2s_raw)
         spread = {V1: held("spread_v", [P, T], F32), S1: held("spread_s1", [P, T], F32)}
         spread[V2] = held("spread_v2", [P, T], F32)
         for t in (V1, S1):
@@ -149,35 +151,48 @@ def tile_moe_mod_silu_kernel(
         def on_vector(window, idx, part, left, right, op):
             nc.vector.tensor_tensor(window[:].indirect(entries(idx, part)), left[:, part], right[:, part], op)
 
-        def on_scalar(window, idx, values, pieces=SCALAR_PIECES):
-            for lo, hi in pieces:
+        def on_scalar(window, idx, values):
+            for lo, hi in SCALAR_PIECES:
                 part = slice(lo, hi)
                 nc.scalar.activation(window[:].indirect(entries(idx, part)), values[:, part], COPY)
 
-        def in_place(tile, part, other, op):
-            nc.vector.tensor_tensor(tile[:, part], tile[:, part], other[:, part], op)
+        def gate_banks(rows):
+            banks = [psum.tile([P, BANK], F32, name=f"bank{BANKS + h}") for h in range(2)]
+            for h in range(2):
+                for i in range(PACK):
+                    nc.tensor.transpose(
+                        banks[h][:, i * P : (i + 1) * P], rows[:, h, i : i + 1].to_broadcast([P, P]), ident[:]
+                    )
+            return banks
 
-        everything = slice(0, S)
-        passes1 = tuple((t, 0, 1) for t in (V1, S1, S2, V2))
-        passes1 = passes1 + tuple((t, c, n) for t in (S1, V1, S2, V2) for c, n in ((1, 2), (3, 1)))
+        def gate_on_vector(banks, dst, src, c, n):
+            gate = banks[c // 2][:].rearrange("p (i j) -> p j i", i=PACK)[:, cols(c % 2, n).start // PACK : cols(c % 2, n).stop // PACK]
+            nc.vector.tensor_tensor(
+                dst[:, cols(c, n)].rearrange("p (j i) -> p j i", i=PACK),
+                src[:, cols(c, n)].rearrange("p (j i) -> p j i", i=PACK),
+                gate,
+                MULT,
+            )
+
+        passes1 = tuple((t, 0, 1) for t in (V1, S1, V2, S2))
+        passes1 = passes1 + tuple((t, c, n) for t in (S1, V1, V2, S2) for c, n in ((1, 2), (3, 1)))
         products(((i % BANKS, one) for i, one in enumerate(passes1)), w1_q, w1_s, gw, gs, y)
         on_vector(spread[V1], idx1, cols(0), y[V1], g1, MULT)
-        in_place(y[S1], everything, g1, MULT)
+        nc.vector.tensor_tensor(y[S1][:], y[S1][:], g1[:], MULT)
         rest = cols(1, NCH - 1)
         gated_v1 = held("gated_v1", [P, S], F32)
         nc.vector.tensor_tensor(gated_v1[:, rest], y[V1][:, rest], g1[:, rest], MULT)
         nc.vector.tensor_copy(spread[V1][:].indirect(entries(idx1, rest)), gated_v1[:, rest])
         on_scalar(spread[S1], idx1, y[S1])
-        nc.gpsimd.tensor_tensor(y[V1][:], y[S2][:], g1[:], MULT)
-        on_scalar(spread[S2], idx1, y[V1])
-        r = {S1: held("r_s1", [P, T], F32)}
-        nc.gpsimd.tensor_tensor(r[S1][:, S:], y[V2][:], g1[:], MULT)
-        nc.vector.tensor_copy(spread[V2][:].indirect(idx1[:]), r[S1][:, S:])
-        r[V1] = held("r_v1", [P, T], F32)
+        nc.gpsimd.tensor_tensor(y[V1][:], y[V2][:], g1[:], MULT)
+        nc.vector.tensor_copy(spread[V2][:].indirect(idx1[:]), y[V1][:])
+        nc.gpsimd.tensor_tensor(y[V2][:], y[S2][:], g1[:], MULT)
+        on_scalar(spread[S2], idx1, y[V2])
+        r = {V1: held("r_v1", [P, T], F32, "g1")}
         nc.gpsimd.tensor_tensor(r[V1][:], res[V1], spread[V1][:], ADD)
-        nc.gpsimd.tensor_tensor(r[S1][:, :SHARE], res[S1][:, :SHARE], spread[S1][:, :SHARE], ADD)
-        nc.vector.tensor_tensor(r[S1][:, SHARE:], res[S1][:, SHARE:], spread[S1][:, SHARE:], ADD)
+        r[S1] = held("r_s1", [P, T], F32, f"res{V1}")
         r[V2] = held("r_v2", [P, T], F32, "spread_v")
+        nc.vector.tensor_tensor(r[S1][:], res[S1], spread[S1][:], ADD)
         r[S2] = held("r_s2", [P, T], F32, f"res{S1}")
         for t in (V2, S2):
             nc.vector.tensor_tensor(r[t][:], res[t], spread[t][:], ADD)
@@ -195,19 +210,9 @@ def tile_moe_mod_silu_kernel(
                     rg[:, :, cols(c)].rearrange("p t (s i) -> p s t i", i=4),
                 )
                 nc.vector.quantize_mx(out=rq[:, cols(c)].bitcast(FP8X4), scales=rs[:, cols(c)], in_=rb[c][:])
-        needed = ((V1, 0), (S1, 0), (S2, 0), (S1, 1), (V1, 1), (V2, 0), (S2, 1), (V2, 1))
-        passes2 = ((V1, 0, 1), (V1, 1, 1)) + tuple((t, 2 * h, 2) for t, h in needed[1:])
+        passes2 = ((V1, 0, 1), (V1, 1, 1), (S1, 0, 2), (S2, 0, 2), (V1, 2, 2), (S1, 2, 2), (V2, 0, 2), (S2, 2, 2), (V2, 2, 2))
         products(zip((0, 5, 1, 2, 3, 4, 3, 5, 0), passes2), w2_q, w2_s, rq, rs, z)
-        g2_banks = [psum.tile([P, BANK], F32, name=f"g2_bank{h}") for h in range(2)]
-        for h in range(2):
-            for i in range(PACK):
-                nc.tensor.transpose(
-                    g2_banks[h][:, i * P : (i + 1) * P], g2_rows[:, h, i : i + 1].to_broadcast([P, P]), ident[:]
-                )
-
-        def gate_on_vector(t, h):
-            values = z[t][:, halves[h]].rearrange("p (j i) -> p j i", i=PACK)
-            nc.vector.tensor_tensor(values, values, g2_banks[h][:].rearrange("p (i j) -> p j i", i=PACK), MULT)
+        g2_banks = gate_banks(g2_rows)
 
         def on_gpsimd(t, part, other, op):
             nc.gpsimd.tensor_tensor(z[t][:, part], z[t][:, part], other[:, part], op)
@@ -215,22 +220,23 @@ def tile_moe_mod_silu_kernel(
         def copy_on_vector(t, part):
             nc.vector.tensor_copy(r[t][:].indirect(entries(idx2, part)), z[t][:, part])
 
-        for t, h in needed[:-2]:
-            gate_on_vector(t, h)
-        for t, h in needed[:-3]:
+        lower, upper = halves
+        needed = ((V1, 0), (S1, 0), (V1, 1), (S1, 1), (S2, 0), (V2, 0))
+        for t, h in needed:
+            gate_on_vector(g2_banks, z[t], z[t], 2 * h, 2)
+        for t, h in needed[:4]:
             on_gpsimd(t, halves[h], rg[:, t, :], ADD)
         on_scalar(r[S1], idx2, z[S1])
-        for part in (cols(0), cols(1), halves[1]):
+        for part in (cols(0), cols(1), upper):
             copy_on_vector(V1, part)
-        between = rg[:, V1, halves[1]]
-        nc.gpsimd.tensor_tensor(between, z[S2][:, halves[1]], g2[:, halves[1]], MULT)
-        on_gpsimd(V2, halves[0], rg[:, V2, :], ADD)
-        nc.gpsimd.tensor_tensor(z[S2][:, halves[1]], between, rg[:, S2, halves[1]], ADD)
-        on_gpsimd(V2, halves[1], g2, MULT)
-        on_gpsimd(V2, halves[1], rg[:, V2, :], ADD)
-        on_scalar(r[S2], idx2, z[S2], CHUNKS)
-        for half in halves:
-            copy_on_vector(V2, half)
+        nc.gpsimd.tensor_tensor(rg[:, S1, upper], z[S2][:, lower], rg[:, S2, lower], ADD)
+        nc.gpsimd.tensor_tensor(rg[:, S2, lower], z[V2][:, lower], rg[:, V2, lower], ADD)
+        nc.gpsimd.tensor_tensor(z[V2][:, lower], z[S2][:, upper], g2[:, upper], MULT)
+        nc.gpsimd.tensor_tensor(rg[:, V2, lower], z[V2][:, lower], rg[:, S2, upper], ADD)
+        nc.gpsimd.tensor_tensor(rg[:, S2, upper], z[V2][:, upper], g2[:, upper], MULT)
+        on_scalar(r[S2], idx2, rg_flat[:, S1 * S + HALF : V2 * S + HALF])
+        nc.vector.tensor_copy(r[V2][:].indirect(entries(idx2, lower)), rg[:, S2, lower])
+        nc.vector.tensor_tensor(r[V2][:].indirect(entries(idx2, upper)), rg[:, S2, upper], rg[:, V2, upper], ADD)
         for t in (S1, S2):
             nc.scalar.dma_start(out_v[:, t, :], r[t][:])
         for t in (V1, V2):

@@ -29,6 +29,7 @@ FLOPS = 2 * 2 * K * K * S
 V1, S1, V2, S2 = 0, 1, 2, 3
 WIDE = 384
 SCALAR_PIECES = ((0, WIDE), (WIDE, 2 * WIDE), (2 * WIDE, S))
+CHUNKS = tuple((c * CH, (c + 1) * CH) for c in range(NCH))
 
 
 def tile_moe_mod_silu_kernel(
@@ -151,8 +152,8 @@ def tile_moe_mod_silu_kernel(
         def on_vector(window, idx, part, left, right, op):
             nc.vector.tensor_tensor(window[:].indirect(entries(idx, part)), left[:, part], right[:, part], op)
 
-        def on_scalar(window, idx, values):
-            for lo, hi in SCALAR_PIECES:
+        def on_scalar(window, idx, values, pieces=SCALAR_PIECES):
+            for lo, hi in pieces:
                 part = slice(lo, hi)
                 nc.scalar.activation(window[:].indirect(entries(idx, part)), values[:, part], COPY)
 
@@ -210,32 +211,33 @@ def tile_moe_mod_silu_kernel(
                     rg[:, :, cols(c)].rearrange("p t (s i) -> p s t i", i=4),
                 )
                 nc.vector.quantize_mx(out=rq[:, cols(c)].bitcast(FP8X4), scales=rs[:, cols(c)], in_=rb[c][:])
-        passes2 = ((V1, 0, 1), (V1, 1, 1), (S1, 0, 2), (S2, 0, 2), (V1, 2, 2), (S1, 2, 2), (V2, 0, 2), (S2, 2, 2), (V2, 2, 2))
+        passes2 = ((V1, 0, 1), (V1, 1, 1), (S1, 0, 2), (S2, 0, 2), (S1, 2, 2), (V1, 2, 2), (V2, 0, 2), (S2, 2, 2), (V2, 2, 2))
         products(zip((0, 5, 1, 2, 3, 4, 3, 5, 0), passes2), w2_q, w2_s, rq, rs, z)
         g2_banks = gate_banks(g2_rows)
 
-        def on_gpsimd(t, part, other, op):
-            nc.gpsimd.tensor_tensor(z[t][:, part], z[t][:, part], other[:, part], op)
-
-        def copy_on_vector(t, part):
-            nc.vector.tensor_copy(r[t][:].indirect(entries(idx2, part)), z[t][:, part])
+        def copy_on_vector(t, part, values):
+            nc.vector.tensor_copy(r[t][:].indirect(entries(idx2, part)), values)
 
         lower, upper = halves
-        needed = ((V1, 0), (S1, 0), (V1, 1), (S1, 1), (S2, 0), (V2, 0))
+        needed = ((V1, 0), (S1, 0), (S1, 1), (S2, 0), (V1, 1), (V2, 0))
         for t, h in needed:
             gate_on_vector(g2_banks, z[t], z[t], 2 * h, 2)
-        for t, h in needed[:4]:
-            on_gpsimd(t, halves[h], rg[:, t, :], ADD)
-        on_scalar(r[S1], idx2, z[S1])
-        for part in (cols(0), cols(1), upper):
-            copy_on_vector(V1, part)
+        for t, h in needed[:3]:
+            nc.gpsimd.tensor_tensor(z[t][:, halves[h]], z[t][:, halves[h]], rg[:, t, halves[h]], ADD)
         nc.gpsimd.tensor_tensor(rg[:, S1, upper], z[S2][:, lower], rg[:, S2, lower], ADD)
-        nc.gpsimd.tensor_tensor(rg[:, S2, lower], z[V2][:, lower], rg[:, V2, lower], ADD)
+        nc.gpsimd.tensor_tensor(rg[:, S2, lower], z[V1][:, upper], rg[:, V1, upper], ADD)
+        nc.gpsimd.tensor_tensor(rg[:, V1, upper], z[V2][:, lower], rg[:, V2, lower], ADD)
         nc.gpsimd.tensor_tensor(z[V2][:, lower], z[S2][:, upper], g2[:, upper], MULT)
         nc.gpsimd.tensor_tensor(rg[:, V2, lower], z[V2][:, lower], rg[:, S2, upper], ADD)
         nc.gpsimd.tensor_tensor(rg[:, S2, upper], z[V2][:, upper], g2[:, upper], MULT)
-        on_scalar(r[S2], idx2, rg_flat[:, S1 * S + HALF : V2 * S + HALF])
-        nc.vector.tensor_copy(r[V2][:].indirect(entries(idx2, lower)), rg[:, S2, lower])
+        values_s2 = rg_flat[:, S1 * S + HALF : V2 * S + HALF]
+        on_scalar(r[S1], idx2, z[S1])
+        for c in range(2):
+            copy_on_vector(V1, cols(c), z[V1][:, cols(c)])
+        copy_on_vector(S2, cols(0), values_s2[:, cols(0)])
+        copy_on_vector(V1, upper, rg[:, S2, lower])
+        on_scalar(r[S2], idx2, values_s2, CHUNKS[1:])
+        copy_on_vector(V2, lower, rg[:, V1, upper])
         nc.vector.tensor_tensor(r[V2][:].indirect(entries(idx2, upper)), rg[:, S2, upper], rg[:, V2, upper], ADD)
         for t in (S1, S2):
             nc.scalar.dma_start(out_v[:, t, :], r[t][:])

from contextlib import ExitStack

import concourse.mybir as mybir
from concourse.masks import make_identity

F32 = mybir.dt.float32
BF16 = mybir.dt.bfloat16
I32 = mybir.dt.int32
U32 = mybir.dt.uint32
U16 = mybir.dt.uint16
U8 = mybir.dt.uint8
FP8X4 = mybir.dt.float8_e4m3fn_x4
MULT = mybir.AluOpType.mult
ADD = mybir.AluOpType.add
SILU = mybir.ActivationFunctionType.Silu
COPY = mybir.ActivationFunctionType.Copy

P = 128
K = 512
T = 2048
S = 1024
PACK = 4
CH = 256
NCH = S // CH
BANK = 512
BANKS = 6
HALF = S // 2
FLOPS = 2 * 2 * K * K * S
V1, S1, V2, S2 = 0, 1, 2, 3
WIDE = 384
SCALAR_PIECES = ((0, WIDE), (WIDE, 2 * WIDE), (2 * WIDE, S))
CHUNKS = tuple((c * CH, (c + 1) * CH) for c in range(NCH))


def tile_moe_mod_silu_kernel(
    tc, x_words, x_scales, xr, w1, w2_words, w2_scales, gate1, gate2, offs, offs2, out
):
    nc = tc.nc
    with ExitStack() as ctx:
        keep = ctx.enter_context(tc.tile_pool(name="keep", bufs=1))
        psum = ctx.enter_context(tc.psum_pool(name="psum", bufs=1))

        def held(name, shape, dtype, tag=None):
            return keep.tile(shape, dtype, name=name, tag=tag or name, align_bytes=64)

        idx1 = keep.tile([P, S // 16], U16, name="idx1")
        idx2 = keep.tile([P, S // 16], U16, name="idx2")
        xw = held("xw", [P, T], I32)
        xs = held("xs", [P, T], U8)
        w1_raw = [held(f"w1_raw{h}", [P, PACK, K // 2], F32) for h in range(2)]
        w1_bf = held("w1_bf", [P, PACK * K], BF16)
        w1_q = held("w1_q", [P, K], U32)
        w1_s = held("w1_s", [P, K], U8)
        w2_raw = held("w2_raw", [P, K], I32)
        w2s_raw = held("w2s_raw", [P, K], U8)
        g1 = held("g1", [P, S], F32)
        g2 = held("g2", [P, S], F32)
        g2_rows = held("g2_rows", [P, 2, PACK], F32)
        ident = held("ident", [P, P], F32)
        zero = held("zero", [P, 2], F32)
        rg_flat = held("rg", [P, PACK * S], F32)
        rg = rg_flat[:].rearrange("p (t s) -> p t s", t=PACK)
        res = {t: held(f"res{t}", [P, T], F32)[:] for t in (V1, S1, V2)}
        res[S2] = rg_flat[:, V2 * S :]
        gs = held("gs", [P, S], U8)
        y = [held(f"y{t}", [P, S], F32) for t in range(PACK)]
        z = [held(f"z{t}", [P, S], F32) for t in range(PACK)]
        rb = [held(f"rb{c}", [P, CH * PACK], BF16) for c in range(NCH)]
        rq = held("rq", [P, S], U32)
        rs = held("rs", [P, S], U8)

        xr_v = xr.rearrange("(p t) c -> p t c", t=PACK)
        out_v = out.rearrange("(p t) c -> p t c", t=PACK)
        w1_v = w1.rearrange("(p j) n -> p j n", j=PACK)

        def cols(c, n=1):
            return slice(c * CH, (c + n) * CH)

        def entries(idx, part):
            return idx[:, part.start // 16 : part.stop // 16]

        def load_scale_rows(scale_tile, rows):
            for q in range(4):
                nc.sync.dma_start(
                    scale_tile[32 * q : 32 * q + 4, :].bitcast(I32), rows[0, 4 * q : 4 * q + 4, :].bitcast(I32)
                )

        nc.gpsimd.memset(xs[:].bitcast(I32), 0)
        nc.sync.dma_start(w1_raw[0][:], w1_v[:, :, : K // 2])
        nc.sync.dma_start(idx1[:], offs)
        load_scale_rows(xs, x_scales)
        nc.vector.memset(zero[:, 0:1], 0.0)
        nc.scalar.activation(zero[:, 1:2], zero[:, 0:1], SILU)
        nc.sync.dma_start(w1_raw[1][:], w1_v[:, :, K // 2 :])
        nc.sync.dma_start(xw[:], x_words[0].rearrange("p c d -> p (c d)").bitcast(I32))
        nc.sync.dma_start(g1[:, cols(0)], gate1[:, cols(0)])
        nc.vector.memset(w2s_raw[:].bitcast(I32), 0)
        nc.sync.dma_start(w2_raw[:], w2_words[0].rearrange("p n d -> p (n d)").bitcast(I32))
        load_scale_rows(w2s_raw, w2_scales)
        nc.sync.dma_start(g1[:, cols(1, NCH - 1)], gate1[:, cols(1, NCH - 1)])

        def to_planes(dst, src):
            nc.gpsimd.tensor_copy(
                dst[:].rearrange("p (t m) -> p t m", t=PACK), src[:].rearrange("p (m t) -> p t m", t=PACK)
            )

        w2_q = held("w2_q", [P, K], I32)
        w2_s = held("w2_s", [P, K], U8)
        to_planes(w2_q, w2_raw)
        to_planes(w2_s, w2s_raw)
        spread = {V1: held("spread_v", [P, T], F32), S1: held("spread_s1", [P, T], F32)}
        spread[V2] = held("spread_v2", [P, T], F32)
        for t in (V1, S1):
            nc.gpsimd.memset(spread[t][:], 0.0)
        nc.scalar.copy(spread[V2][:, :S], zero[:, 1:2].to_broadcast([P, S]))
        nc.gpsimd.memset(spread[V2][:, S:], 0.0)
        make_identity(nc, ident[:])
        for t in (V1, S1, V2, S2):
            nc.sync.dma_start(res[t], xr_v[:, t, :])
        nc.sync.dma_start(idx2[:], offs2)
        nc.sync.dma_start(g2[:, HALF:], gate2[:, HALF:])
        nc.sync.dma_start(g2_rows[:], gate2[0].rearrange("(h j i) -> j h i", h=2, i=PACK))

        nc.vector.tensor_copy(gs[:], xs[:].indirect(idx1[:]))
        w1_dst = w1_bf[:].rearrange("p (t m j) -> p m t j", t=PACK, j=PACK)
        for h in range(2):
            nc.scalar.copy(
                w1_dst[:, P // 2 * h : P // 2 * (h + 1)], w1_raw[h][:].rearrange("p j (m t) -> p m t j", t=PACK)
            )
        nc.vector.quantize_mx(out=w1_q[:].bitcast(FP8X4), scales=w1_s[:], in_=w1_bf[:])
        gw = held("gw", [P, S], U32, "w1_bf")
        for c, n in ((0, 1), (1, NCH - 1)):
            nc.vector.tensor_copy(gw[:, cols(c, n)], xw[:].bitcast(U32).indirect(entries(idx1, cols(c, n))))
        spread[S2] = held("spread_s2", [P, T], F32, "xw")
        nc.gpsimd.memset(spread[S2][:], 0.0)

        def products(passes, wq, ws, codes, scales, dst):
            for i, (t, c, n) in passes:
                acc = psum.tile([P, BANK], F32, name=f"bank{i}")
                w_cols = slice(t * P, (t + 1) * P)
                nc.tensor.matmul_mx(
                    out=acc[:, : n * CH],
                    lhsT=wq[:, w_cols].bitcast(FP8X4),
                    lhsT_scale=ws[:, w_cols],
                    rhs=codes[:, cols(c, n)].bitcast(FP8X4),
                    rhs_scale=scales[:, cols(c, n)],
                    start=True,
                    stop=True,
                )
                nc.scalar.activation(dst[t][:, cols(c, n)], acc[:, : n * CH], SILU)

        def on_vector(window, idx, part, left, right, op):
            nc.vector.tensor_tensor(window[:].indirect(entries(idx, part)), left[:, part], right[:, part], op)

        def on_scalar(window, idx, values, pieces=SCALAR_PIECES):
            for lo, hi in pieces:
                part = slice(lo, hi)
                nc.scalar.activation(window[:].indirect(entries(idx, part)), values[:, part], COPY)

        def gate_banks(rows):
            banks = [psum.tile([P, BANK], F32, name=f"bank{BANKS + h}") for h in range(2)]
            for h in range(2):
                for i in range(PACK):
                    nc.tensor.transpose(
                        banks[h][:, i * P : (i + 1) * P], rows[:, h, i : i + 1].to_broadcast([P, P]), ident[:]
                    )
            return banks

        def gate_on_vector(banks, dst, src, c, n):
            gate = banks[c // 2][:].rearrange("p (i j) -> p j i", i=PACK)[:, cols(c % 2, n).start // PACK : cols(c % 2, n).stop // PACK]
            nc.vector.tensor_tensor(
                dst[:, cols(c, n)].rearrange("p (j i) -> p j i", i=PACK),
                src[:, cols(c, n)].rearrange("p (j i) -> p j i", i=PACK),
                gate,
                MULT,
            )

        passes1 = tuple((t, 0, 1) for t in (V1, S1, V2, S2))
        passes1 = passes1 + tuple((t, c, n) for t in (S1, V1, V2, S2) for c, n in ((1, 2), (3, 1)))
        products(((i % BANKS, one) for i, one in enumerate(passes1)), w1_q, w1_s, gw, gs, y)
        on_vector(spread[V1], idx1, cols(0), y[V1], g1, MULT)
        nc.vector.tensor_tensor(y[S1][:], y[S1][:], g1[:], MULT)
        rest = cols(1, NCH - 1)
        gated_v1 = held("gated_v1", [P, S], F32)
        nc.vector.tensor_tensor(gated_v1[:, rest], y[V1][:, rest], g1[:, rest], MULT)
        nc.vector.tensor_copy(spread[V1][:].indirect(entries(idx1, rest)), gated_v1[:, rest])
        on_scalar(spread[S1], idx1, y[S1])
        nc.gpsimd.tensor_tensor(y[V1][:], y[V2][:], g1[:], MULT)
        nc.vector.tensor_copy(spread[V2][:].indirect(idx1[:]), y[V1][:])
        nc.gpsimd.tensor_tensor(y[V2][:], y[S2][:], g1[:], MULT)
        on_scalar(spread[S2], idx1, y[V2])
        r = {V1: held("r_v1", [P, T], F32, "g1")}
        nc.gpsimd.tensor_tensor(r[V1][:], res[V1], spread[V1][:], ADD)
        r[S1] = held("r_s1", [P, T], F32, f"res{V1}")
        r[V2] = held("r_v2", [P, T], F32, "spread_v")
        nc.vector.tensor_tensor(r[S1][:], res[S1], spread[S1][:], ADD)
        r[S2] = held("r_s2", [P, T], F32, f"res{S1}")
        for t in (V2, S2):
            nc.vector.tensor_tensor(r[t][:], res[t], spread[t][:], ADD)

        halves = (cols(0, 2), cols(2, 2))
        for t in (V1, S1):
            nc.scalar.activation(rg[:, t, :], r[t][:].indirect(idx2[:]), COPY)
        nc.vector.tensor_copy(rg[:, V2, :], r[V2][:].indirect(idx2[:]))
        for h, half in enumerate(halves):
            nc.scalar.activation(rg[:, S2, half], r[S2][:].indirect(entries(idx2, half)), COPY)
            for c in (2 * h, 2 * h + 1):
                cast = nc.scalar.copy if c == NCH - 1 else nc.vector.tensor_copy
                cast(
                    rb[c][:].rearrange("p (s i t) -> p s t i", i=4, t=PACK),
                    rg[:, :, cols(c)].rearrange("p t (s i) -> p s t i", i=4),
                )
                nc.vector.quantize_mx(out=rq[:, cols(c)].bitcast(FP8X4), scales=rs[:, cols(c)], in_=rb[c][:])
        passes2 = ((V1, 0, 1), (V1, 1, 1), (S1, 0, 2), (S2, 0, 2), (S1, 2, 2), (V1, 2, 2), (V2, 0, 2), (S2, 2, 2), (V2, 2, 2))
        products(zip((0, 5, 1, 2, 3, 4, 3, 5, 0), passes2), w2_q, w2_s, rq, rs, z)
        g2_banks = gate_banks(g2_rows)

        def copy_on_vector(t, part, values):
            nc.vector.tensor_copy(r[t][:].indirect(entries(idx2, part)), values)

        lower, upper = halves
        needed = ((V1, 0), (S1, 0), (S1, 1), (S2, 0), (V1, 1), (V2, 0))
        for t, h in needed:
            gate_on_vector(g2_banks, z[t], z[t], 2 * h, 2)
        for t, h in needed[:3]:
            nc.gpsimd.tensor_tensor(z[t][:, halves[h]], z[t][:, halves[h]], rg[:, t, halves[h]], ADD)
        nc.gpsimd.tensor_tensor(rg[:, S1, upper], z[S2][:, lower], rg[:, S2, lower], ADD)
        nc.gpsimd.tensor_tensor(rg[:, S2, lower], z[V1][:, upper], rg[:, V1, upper], ADD)
        nc.gpsimd.tensor_tensor(rg[:, V1, upper], z[V2][:, lower], rg[:, V2, lower], ADD)
        nc.gpsimd.tensor_tensor(z[V2][:, lower], z[S2][:, upper], g2[:, upper], MULT)
        nc.gpsimd.tensor_tensor(rg[:, V2, lower], z[V2][:, lower], rg[:, S2, upper], ADD)
        nc.gpsimd.tensor_tensor(rg[:, S2, upper], z[V2][:, upper], g2[:, upper], MULT)
        values_s2 = rg_flat[:, S1 * S + HALF : V2 * S + HALF]
        on_scalar(r[S1], idx2, z[S1])
        for c in range(2):
            copy_on_vector(V1, cols(c), z[V1][:, cols(c)])
        copy_on_vector(S2, cols(0), values_s2[:, cols(0)])
        copy_on_vector(V1, upper, rg[:, S2, lower])
        on_scalar(r[S2], idx2, values_s2, CHUNKS[1:])
        copy_on_vector(V2, lower, rg[:, V1, upper])
        nc.vector.tensor_tensor(r[V2][:].indirect(entries(idx2, upper)), rg[:, S2, upper], rg[:, V2, upper], ADD)
        for t in (S1, S2):
            nc.scalar.dma_start(out_v[:, t, :], r[t][:])
        for t in (V1, V2):
            nc.sync.dma_start(out_v[:, t, :], r[t][:])
